import numpy as np
import ml_dtypes


def mxq(x, axis, fmt="e4m3"):
    dtype, down = {"e4m3": (ml_dtypes.float8_e4m3fn, 7), "e5m2": (ml_dtypes.float8_e5m2, 14)}[fmt]
    v = np.moveaxis(np.asarray(x, np.float32).astype(ml_dtypes.bfloat16).astype(np.float64), axis, -1)
    blocks = v.reshape(v.shape[:-1] + (-1, 32))
    amax = np.abs(blocks).max(-1, keepdims=True)
    byte = np.maximum(np.where(amax > 0, np.frexp(amax)[1] - 1 + 127, 0) - down, 1)
    scale = np.exp2(byte - 127.0)
    codes = (blocks / scale).astype(np.float32).astype(dtype).astype(np.float64)
    return np.moveaxis((codes * scale).reshape(v.shape), -1, axis)


WIDE = False


def mx_kscale(k):
    if not WIDE:
        return np.ones(k)
    levels = np.array([10, -10, 5, -5, 0])
    if k % 512:
        return np.exp2(np.random.permutation(np.resize(levels, k // 32))).repeat(32)
    a = np.empty((k // 512, 16))
    for p in range(k // 512):
        a[p, :8] = np.random.permutation(np.resize(levels, 8))
        for g in range(8):
            far = levels[np.abs(levels - a[p, g]) >= 10]
            a[p, g + 8] = far[np.random.randint(len(far))]
    return np.exp2(a.ravel()).repeat(32)


def f64(x):
    return np.asarray(x).astype(np.float64)


def striped(idx):
    return np.tile(idx.reshape(-1, 16).T, (8, 1)).astype(np.uint16)


def unstriped(offs):
    return offs[:16].T.reshape(-1).astype(np.int64)


E2M1 = np.array([0.0, 0.5, 1.0, 1.5, 2.0, 3.0, 4.0, 6.0, -0.0, -0.5, -1.0, -1.5, -2.0, -3.0, -4.0, -6.0])


def pack_weight(w, fmt):
    k, n = w.shape
    w = f64(np.asarray(w, np.float32).astype(ml_dtypes.bfloat16)).reshape(k // 32, 32, n)
    amax = np.abs(w).max(1)
    if fmt == "e4m3":
        byte = np.frexp(amax)[1] - 1 + 127 - 7
    else:
        mant, ex = np.frexp(amax / 6.0)
        byte = np.where(mant > 0.5, ex, ex - 1) + 127
    byte = np.clip(np.where(amax > 0, byte, 1), 1, 254)
    scaled = (w * np.exp2(127.0 - byte)[:, None, :]).reshape(k, n).astype(np.float32)
    by_word = np.ascontiguousarray(scaled.reshape(k // 512, 128, 4, n).transpose(0, 1, 3, 2))
    if fmt == "e4m3":
        words = by_word.astype(ml_dtypes.float8_e4m3fn).view(np.uint8)
    else:
        c = by_word.astype(ml_dtypes.float4_e2m1fn).view(np.uint8) & 0xF
        words = (c[..., 0::2] | (c[..., 1::2] << 4)).reshape(k // 512, 128, 2 * n)
    return np.ascontiguousarray(words), np.ascontiguousarray(byte.astype(np.uint8).reshape(k // 512, 16, n))


def unpack_weight(words, scales, fmt):
    g, _, n = scales.shape
    words = np.ascontiguousarray(words).reshape(g, 128, n, -1)
    if fmt == "e4m3":
        vals = words.view(ml_dtypes.float8_e4m3fn).astype(np.float64)
    else:
        nib = np.empty((g, 128, n, 4), np.uint8)
        nib[..., 0::2] = words & 0xF
        nib[..., 1::2] = words >> 4
        vals = E2M1[nib]
    vals = vals * np.repeat(np.exp2(scales.astype(np.float64) - 127.0), 8, axis=1)[..., None]
    return vals.transpose(0, 1, 3, 2).reshape(g * 512, n)


def relu(v):
    return np.maximum(v, 0.0)


K, T, E, C, H, N = 512, 768, 9, 256, 512, 256
TOP = 3


def by_expert(wq, xq):
    return np.concatenate([wq[e].T @ xq[:, e * C:(e + 1) * C] for e in range(E)], axis=1)


def setup_inputs():
    n = np.random.standard_normal
    s = mx_kscale(K)[:, None]
    u = mx_kscale(H)
    deal = np.repeat(np.arange(E), C).reshape(TOP, T)[:, np.random.permutation(T)]
    deal = np.take_along_axis(deal, np.argsort(np.random.rand(TOP, T), axis=0), axis=0)
    for _ in range(8):
        s_, t_ = np.random.permutation(T).reshape(2, -1); r = np.random.randint(TOP, size=T // 2); x, y = deal[r, s_].copy(), deal[r, t_].copy()
        ok = ~((deal[:, s_] == y).any(0) | (deal[:, t_] == x).any(0)); deal[r[ok], s_[ok]] = y[ok]; deal[r[ok], t_[ok]] = x[ok]
    order = np.lexsort((np.random.rand(TOP * T), deal.reshape(-1)))
    slot_token = order % T; pos = np.empty(TOP * T, np.int64); pos[order] = np.arange(TOP * T); pos = pos.reshape(TOP, T)
    g = np.random.uniform(0.5, 1.5, (TOP, T)); g = g / g.sum(0)
    w1 = [pack_weight(m, "e2m1") for m in n((E, K, H)) / np.sqrt(K) / s[None] * u[None, None, :]]
    w2 = [pack_weight(m, "e2m1") for m in n((E, H, N)) / np.sqrt(H) / u[None, :, None]]
    x = pack_weight(n((K, T)) * s, "e4m3")
    return {
        "x_words": x[0],
        "x_scales": x[1],
        "w1_words": np.stack([m[0] for m in w1]),
        "w1_scales": np.stack([m[1] for m in w1]),
        "w2_words": np.stack([m[0] for m in w2]),
        "w2_scales": np.stack([m[1] for m in w2]),
        "gate": np.stack([np.tile(r, (N, 1)) for r in g]).astype(np.float32),
        "offs": striped(slot_token),
        "pos1": striped(pos[0]),
        "pos2": striped(pos[1]),
        "pos3": striped(pos[2]),
    }


def reference(x_words, x_scales, w1_words, w1_scales, w2_words, w2_scales, gate, offs, pos1, pos2, pos3):
    idx = unstriped(offs)
    w1 = np.stack([unpack_weight(w1_words[e], w1_scales[e], "e2m1") for e in range(E)])
    w2 = np.stack([unpack_weight(w2_words[e], w2_scales[e], "e2m1") for e in range(E)])
    xq = unpack_weight(x_words, x_scales, "e4m3")[:, idx]
    h = relu(by_expert(w1, xq))
    y = by_expert(w2, mxq(h, 0, "e4m3"))
    return sum(f64(gate[r]) * y[:, unstriped(p)] for r, p in enumerate((pos1, pos2, pos3)))

@@ -1,0 +1,185 @@
+from contextlib import ExitStack
+
+import concourse.mybir as mybir
+from concourse.masks import make_identity
+
+K, T, E, C, H, N = 512, 768, 9, 256, 512, 256
+TOP = 3
+S = E * C
+P = 128
+FLOPS = 2 * S * (K * H + H * N)
+
+F32 = mybir.dt.float32
+BF16 = mybir.dt.bfloat16
+I32 = mybir.dt.int32
+U32 = mybir.dt.uint32
+U16 = mybir.dt.uint16
+U8 = mybir.dt.uint8
+FP8X4 = mybir.dt.float8_e4m3fn_x4
+FP4X4 = mybir.dt.float4_e2m1fn_x4
+RELU = mybir.ActivationFunctionType.Relu
+MULT = mybir.AluOpType.mult
+ADD = mybir.AluOpType.add
+
+VECTOR_TURNS = (0, 1, 2, 4, 6, 8)
+TAIL = ((0, 0, 512), (0, 512, 768), (1, 0, 256), (1, 256, 512), (1, 512, 768))
+EARLY = 3
+
+
+def tile_moe_pkd_mlp_relu_kernel(
+    tc, x_words, x_scales, w1_words, w1_scales, w2_words, w2_scales, gate, offs, pos1, pos2, pos3, out
+):
+    nc = tc.nc
+    with ExitStack() as ctx:
+        keep = ctx.enter_context(tc.tile_pool(name="keep", bufs=1))
+        psum_a = ctx.enter_context(tc.psum_pool(name="psum_a", bufs=3))
+        psum_t = ctx.enter_context(tc.psum_pool(name="psum_t", bufs=3))
+        psum_y = ctx.enter_context(tc.psum_pool(name="psum_y", bufs=2))
+
+        offs_sb = keep.tile([P, S // 16], U16, name="offs_sb")
+        pos_sb = [keep.tile([P, T // 16], U16, name=f"pos_sb{r}") for r in range(TOP)]
+        xw = keep.tile([P, T], I32, name="xw", align_bytes=64)
+        xs = keep.tile([P, T], U8, name="xs", align_bytes=64)
+        w1w = keep.tile([P, E * 2 * H], U8, name="w1w", align_bytes=64)
+        w1s = keep.tile([P, E * H], U8, name="w1s", align_bytes=64)
+        w2w = keep.tile([P, E * 2 * N], U8, name="w2w", align_bytes=64)
+        w2s = keep.tile([P, E * N], U8, name="w2s", align_bytes=64)
+        gate_sb = [[keep.tile([P, T], F32, name=f"gate{h}_{r}") for r in range(TOP)] for h in range(2)]
+        ident = keep.tile([P, P], F32, name="ident")
+        warm = keep.tile([P, 8], F32, name="warm")
+
+        nc.gpsimd.memset(xs[:].bitcast(I32), 0)
+        nc.gpsimd.memset(w1s[:, : EARLY * H].bitcast(I32), 0)
+        nc.vector.memset(warm[:], 0.0)
+        nc.vector.memset(w1s[:, EARLY * H :].bitcast(I32), 0)
+        nc.vector.memset(w2s[:].bitcast(I32), 0)
+        make_identity(nc, ident[:])
+
+        def load_scales(queue, plane, scales, width, e0, e1):
+            for q in range(4):
+                queue.dma_start(
+                    out=plane[32 * q : 32 * q + 4, e0 * width : e1 * width]
+                    .bitcast(I32)
+                    .rearrange("r (e w) -> r e w", w=width // 4),
+                    in_=scales[e0:e1, 4 * q : 4 * q + 4, :].rearrange("e r w -> r e w").bitcast(I32),
+                )
+
+        def load_words(tile, words, width, e0, e1):
+            nc.sync.dma_start(
+                out=tile[:, e0 * width : e1 * width].bitcast(I32).rearrange("p (e w) -> p e w", w=width // 4),
+                in_=words[e0:e1, 0].rearrange("e p w -> p e w").bitcast(I32),
+            )
+
+        nc.sync.dma_start(offs_sb[:], offs)
+        nc.sync.dma_start(out=xw[:], in_=x_words[0].rearrange("p t r -> p (t r)").bitcast(I32))
+        load_scales(nc.scalar, xs, x_scales, T, 0, 1)
+        nc.scalar.activation(warm[:, 4:5], warm[:, 0:1], RELU)
+        load_words(w1w, w1_words, 2 * H, 0, 1)
+        load_scales(nc.sync, w1s, w1_scales[:, 0], H, 0, EARLY)
+        load_words(w1w, w1_words, 2 * H, 1, 3)
+        load_scales(nc.sync, w1s, w1_scales[:, 0], H, EARLY, E)
+        load_words(w1w, w1_words, 2 * H, 3, 6)
+        load_words(w1w, w1_words, 2 * H, 6, 9)
+        load_scales(nc.sync, w2s, w2_scales[:, 0], N, 0, E)
+        load_words(w2w, w2_words, 2 * N, 0, E)
+        for r, pos in enumerate((pos1, pos2, pos3)):
+            nc.sync.dma_start(pos_sb[r][:], pos)
+        for h in range(2):
+            for r in range(TOP):
+                nc.sync.dma_start(out=gate_sb[h][r][:], in_=gate[r, h * P : (h + 1) * P, :])
+
+        h_rows = []
+        for e in range(E):
+            picks = offs_sb[:, e * C // 16 : (e + 1) * C // 16]
+            gw = keep.tile([P, C], U32, name=f"gw{e}", align_bytes=64)
+            gs = keep.tile([P, C], U8, name=f"gs{e}", align_bytes=64)
+            nc.vector.tensor_copy(gw[:], xw[:].bitcast(U32).indirect(picks))
+            nc.vector.tensor_copy(gs[:], xs[:].indirect(picks))
+            hb = keep.tile([P, 2, H], BF16, name=f"hb{e}", align_bytes=64)
+            for b in range(2):
+                acc = psum_a.tile([P, H], F32, name="acc")
+                nc.tensor.matmul_mx(
+                    out=acc[:],
+                    lhsT=gw[:, b * P : (b + 1) * P].bitcast(FP8X4),
+                    lhsT_scale=gs[:, b * P : (b + 1) * P],
+                    rhs=w1w[:, e * 2 * H : (e + 1) * 2 * H].bitcast(FP4X4),
+                    rhs_scale=w1s[:, e * H : (e + 1) * H],
+                    start=True,
+                    stop=True,
+                )
+                nc.scalar.activation(
+                    hb[:, b, :].rearrange("s (u p d) -> s u p d", u=2, d=2),
+                    acc[:].rearrange("s (p u d) -> s u p d", u=2, d=2),
+                    RELU,
+                )
+            h_rows.append(hb)
+
+        y = [keep.tile([P, S], F32, name=f"y{h}") for h in range(2)]
+        hq = [keep.tile([P, C], U32, name=f"hq{e}", align_bytes=64) for e in range(E)]
+        hs = [keep.tile([P, C], U8, name=f"hs{e}", align_bytes=64) for e in range(E)]
+
+        def second_layer(e, h):
+            acc = psum_y.tile([P, C], F32, name="acc_y")
+            col = e * N + h * P
+            nc.tensor.matmul_mx(
+                out=acc[:],
+                lhsT=w2w[:, 2 * col : 2 * (col + P)].bitcast(FP4X4),
+                lhsT_scale=w2s[:, col : col + P],
+                rhs=hq[e][:].bitcast(FP8X4),
+                rhs_scale=hs[e][:],
+                start=True,
+                stop=True,
+            )
+            nc.scalar.copy(y[h][:, e * C : (e + 1) * C], acc[:])
+
+        for e in range(E):
+            words = h_rows[e][:].rearrange("s b i -> s (b i)").bitcast(F32)
+            turned = psum_t.tile([P, 4, P], F32, name="turned")
+            for j in range(4):
+                nc.tensor.transpose(turned[:, j, :], words[:, j * P : (j + 1) * P], ident[:])
+            ht = keep.tile([P, 4 * C], BF16, name=f"ht{e}", align_bytes=64)
+            dst = ht[:].bitcast(F32).rearrange("p (b s u) -> p b s u", b=2, u=2)
+            src = turned[:].rearrange("p (b u) s -> p b s u", u=2)
+            if e in VECTOR_TURNS:
+                nc.vector.tensor_copy(dst, src)
+            else:
+                nc.scalar.copy(dst, src)
+            nc.vector.quantize_mx(out=hq[e][:].bitcast(FP8X4), scales=hs[e][:], in_=ht[:])
+            second_layer(e, 0)
+        for e in range(E):
+            second_layer(e, 1)
+
+        for h, t0, t1 in TAIL:
+            prods = []
+            for r in range(TOP):
+                prod = keep.tile([P, t1 - t0], F32, name=f"prod{h}_{t0}_{r}")
+                nc.vector.tensor_tensor(
+                    prod[:], y[h][:].indirect(pos_sb[r][:, t0 // 16 : t1 // 16]), gate_sb[h][r][:, t0:t1], MULT
+                )
+                prods.append(prod)
+            rows = out[h * P : (h + 1) * P, t0:t1]
+            if (h, t0, t1) == TAIL[-1]:
+                nc.vector.tensor_tensor(prods[0][:], prods[0][:], prods[1][:], ADD)
+                nc.vector.tensor_tensor(prods[2][:], prods[0][:], prods[2][:], ADD)
+                nc.sync.dma_start(out=rows, in_=prods[2][:])
+                continue
+            width = t1 - t0
+            summed = psum_a.tile([P, width], F32, name="acc")
+            for c0 in range(0, width, P):
+                for r in range(TOP):
+                    nc.tensor.matmul(
+                        summed[:, c0 : c0 + P],
+                        lhsT=prods[r][:, c0 : c0 + P],
+                        rhs=ident[:],
+                        is_transpose=True,
+                        start=(r == 0),
+                        stop=(r == TOP - 1),
+                    )
+            by_token = keep.tile([P, width], F32, name=f"by_token{h}_{t0}")
+            nc.scalar.copy(by_token[:], summed[:])
+            back = psum_a.tile([P, width], F32, name="acc")
+            for c0 in range(0, width, P):
+                nc.tensor.transpose(back[:, c0 : c0 + P], by_token[:, c0 : c0 + P], ident[:])
+            result = keep.tile([P, width], F32, name=f"result{h}_{t0}")
+            nc.scalar.copy(result[:], back[:])
+            nc.sync.dma_start(out=rows, in_=result[:])

@@ -21,9 +21,14 @@ RELU = mybir.ActivationFunctionType.Relu
 MULT = mybir.AluOpType.mult
 ADD = mybir.AluOpType.add
 
-VECTOR_TURNS = (0, 1, 2, 4, 6, 8)
-TAIL = ((0, 0, 512), (0, 512, 768), (1, 0, 256), (1, 256, 512), (1, 512, 768))
+GATHER_BLOCKS = (1, 3, 2, 4, 4, 4)
+VECTOR_TURNS = (4, 5, 6)
+PERMUTED = ()
+Y_RUNS = (((0, 1), (2, 3), (4, 5), (6, 7), (8,)), ((0, 1), (2, 3), (4, 5), (6, 7), (8,)))
+VECTOR_Y = (0, 2)
+TAIL = ((0, 0, 384), (0, 384, 768), (1, 0, 256), (1, 256, 512), (1, 512, 768))
 EARLY = 3
+LAG_T, LAG_Q, LAG_Y = 3, 0, 0
 
 
 def tile_moe_pkd_mlp_relu_kernel(
@@ -40,121 +45,184 @@ def tile_moe_pkd_mlp_relu_kernel(
         pos_sb = [keep.tile([P, T // 16], U16, name=f"pos_sb{r}") for r in range(TOP)]
         xw = keep.tile([P, T], I32, name="xw", align_bytes=64)
         xs = keep.tile([P, T], U8, name="xs", align_bytes=64)
-        w1w = keep.tile([P, E * 2 * H], U8, name="w1w", align_bytes=64)
-        w1s = keep.tile([P, E * H], U8, name="w1s", align_bytes=64)
-        w2w = keep.tile([P, E * 2 * N], U8, name="w2w", align_bytes=64)
+        w1s_early = keep.tile([P, EARLY * H], U8, name="w1s_early", align_bytes=64)
+        w1s_late = keep.tile([P, (E - EARLY) * H], U8, name="w1s_late", align_bytes=64)
+        w1s = [w1s_early[:, e * H : (e + 1) * H] for e in range(EARLY)]
+        w1s += [w1s_late[:, e * H : (e + 1) * H] for e in range(E - EARLY)]
         w2s = keep.tile([P, E * N], U8, name="w2s", align_bytes=64)
-        gate_sb = [[keep.tile([P, T], F32, name=f"gate{h}_{r}") for r in range(TOP)] for h in range(2)]
+        gate_sb = [keep.tile([P, T], F32, name=f"gate{j}") for j in range(2 * TOP)]
         ident = keep.tile([P, P], F32, name="ident")
         warm = keep.tile([P, 8], F32, name="warm")
 
-        nc.gpsimd.memset(xs[:].bitcast(I32), 0)
-        nc.gpsimd.memset(w1s[:, : EARLY * H].bitcast(I32), 0)
-        nc.vector.memset(warm[:], 0.0)
-        nc.vector.memset(w1s[:, EARLY * H :].bitcast(I32), 0)
+        nc.vector.memset(w1s_early[:].bitcast(I32), 0)
+        nc.vector.memset(w1s_late[:].bitcast(I32), 0)
         nc.vector.memset(w2s[:].bitcast(I32), 0)
+        nc.gpsimd.memset(warm[:], 0.0)
         make_identity(nc, ident[:])
 
-        def load_scales(queue, plane, scales, width, e0, e1):
+        def load_scales(queues, plane, scales, width, e0, e1):
             for q in range(4):
-                queue.dma_start(
-                    out=plane[32 * q : 32 * q + 4, e0 * width : e1 * width]
-                    .bitcast(I32)
-                    .rearrange("r (e w) -> r e w", w=width // 4),
+                queues[q].dma_start(
+                    out=plane[32 * q : 32 * q + 4, :].bitcast(I32).rearrange("r (e w) -> r e w", w=width // 4),
                     in_=scales[e0:e1, 4 * q : 4 * q + 4, :].rearrange("e r w -> r e w").bitcast(I32),
                 )
 
-        def load_words(tile, words, width, e0, e1):
+        def load_words(words, width, e0, e1, name, tag=""):
+            tile = keep.tile([P, (e1 - e0) * width], U8, name=name, tag=tag, align_bytes=64)
             nc.sync.dma_start(
-                out=tile[:, e0 * width : e1 * width].bitcast(I32).rearrange("p (e w) -> p e w", w=width // 4),
+                out=tile[:].bitcast(I32).rearrange("p (e w) -> p e w", w=width // 4),
                 in_=words[e0:e1, 0].rearrange("e p w -> p e w").bitcast(I32),
             )
+            return [tile[:, j * width : (j + 1) * width] for j in range(e1 - e0)]
 
         nc.sync.dma_start(offs_sb[:], offs)
+        for q in range(4):
+            rows = x_scales[0, 4 * q : 4 * q + 4, :].bitcast(I32)
+            nc.scalar.dma_start(
+                out=xs[32 * q : 32 * q + 32, :].bitcast(I32),
+                in_=rows.unsqueeze(0).broadcast_to([8, 4, T // 4]),
+            )
         nc.sync.dma_start(out=xw[:], in_=x_words[0].rearrange("p t r -> p (t r)").bitcast(I32))
-        load_scales(nc.scalar, xs, x_scales, T, 0, 1)
+        w1w = load_words(w1_words, 2 * H, 0, 1, "w1w_a")
         nc.scalar.activation(warm[:, 4:5], warm[:, 0:1], RELU)
-        load_words(w1w, w1_words, 2 * H, 0, 1)
-        load_scales(nc.sync, w1s, w1_scales[:, 0], H, 0, EARLY)
-        load_words(w1w, w1_words, 2 * H, 1, 3)
-        load_scales(nc.sync, w1s, w1_scales[:, 0], H, EARLY, E)
-        load_words(w1w, w1_words, 2 * H, 3, 6)
-        load_words(w1w, w1_words, 2 * H, 6, 9)
-        load_scales(nc.sync, w2s, w2_scales[:, 0], N, 0, E)
-        load_words(w2w, w2_words, 2 * N, 0, E)
+        load_scales((nc.sync, nc.sync, nc.sync, nc.sync), w1s_early, w1_scales[:, 0], H, 0, EARLY)
+        w1w += load_words(w1_words, 2 * H, 1, 3, "w1w_b")
+        load_scales((nc.sync,) * 4, w1s_late, w1_scales[:, 0], H, EARLY, E)
+        w1w += load_words(w1_words, 2 * H, 3, 6, "w1w_c")
+        w1w += load_words(w1_words, 2 * H, 6, 9, "w1w_d")
+        load_scales((nc.sync,) * 4, w2s, w2_scales[:, 0], N, 0, E)
         for r, pos in enumerate((pos1, pos2, pos3)):
             nc.sync.dma_start(pos_sb[r][:], pos)
-        for h in range(2):
-            for r in range(TOP):
-                nc.sync.dma_start(out=gate_sb[h][r][:], in_=gate[r, h * P : (h + 1) * P, :])
+        w2w = load_words(w2_words, 2 * N, 0, E, "w2w")
+        for j in range(2 * TOP):
+            h, r = divmod(j, TOP)
+            nc.sync.dma_start(out=gate_sb[j][:], in_=gate[r, h * P : (h + 1) * P, :])
 
-        h_rows = []
-        for e in range(E):
-            picks = offs_sb[:, e * C // 16 : (e + 1) * C // 16]
-            gw = keep.tile([P, C], U32, name=f"gw{e}", align_bytes=64)
-            gs = keep.tile([P, C], U8, name=f"gs{e}", align_bytes=64)
-            nc.vector.tensor_copy(gw[:], xw[:].bitcast(U32).indirect(picks))
-            nc.vector.tensor_copy(gs[:], xs[:].indirect(picks))
-            hb = keep.tile([P, 2, H], BF16, name=f"hb{e}", align_bytes=64)
-            for b in range(2):
-                acc = psum_a.tile([P, H], F32, name="acc")
-                nc.tensor.matmul_mx(
-                    out=acc[:],
-                    lhsT=gw[:, b * P : (b + 1) * P].bitcast(FP8X4),
-                    lhsT_scale=gs[:, b * P : (b + 1) * P],
-                    rhs=w1w[:, e * 2 * H : (e + 1) * 2 * H].bitcast(FP4X4),
-                    rhs_scale=w1s[:, e * H : (e + 1) * H],
-                    start=True,
-                    stop=True,
-                )
-                nc.scalar.activation(
-                    hb[:, b, :].rearrange("s (u p d) -> s u p d", u=2, d=2),
-                    acc[:].rearrange("s (p u d) -> s u p d", u=2, d=2),
-                    RELU,
-                )
-            h_rows.append(hb)
-
+        starts = {sum(GATHER_BLOCKS[:g]): g for g in range(len(GATHER_BLOCKS))}
+        gathered = []
+        h_rows, h_cols = {}, {}
+        w2_tiles = [w2w]
         y = [keep.tile([P, S], F32, name=f"y{h}") for h in range(2)]
         hq = [keep.tile([P, C], U32, name=f"hq{e}", align_bytes=64) for e in range(E)]
         hs = [keep.tile([P, C], U8, name=f"hs{e}", align_bytes=64) for e in range(E)]
 
-        def second_layer(e, h):
-            acc = psum_y.tile([P, C], F32, name="acc_y")
-            col = e * N + h * P
-            nc.tensor.matmul_mx(
-                out=acc[:],
-                lhsT=w2w[:, 2 * col : 2 * (col + P)].bitcast(FP4X4),
-                lhsT_scale=w2s[:, col : col + P],
-                rhs=hq[e][:].bitcast(FP8X4),
-                rhs_scale=hs[e][:],
-                start=True,
-                stop=True,
-            )
-            nc.scalar.copy(y[h][:, e * C : (e + 1) * C], acc[:])
+        def gather(block):
+            g = starts[block]
+            width = GATHER_BLOCKS[g] * P
+            picks = offs_sb[:, block * P // 16 : (block * P + width) // 16]
+            gw = keep.tile([P, width], U32, name=f"gw{g}", tag=f"gw{g % 2}", align_bytes=64)
+            gs = keep.tile([P, width], U8, name=f"gs{g}", tag=f"gs{g % 2}", align_bytes=64)
+            nc.vector.tensor_copy(gw[:], xw[:].bitcast(U32).indirect(picks))
+            nc.vector.tensor_copy(gs[:], xs[:].indirect(picks))
+            for c0 in range(0, width, P):
+                gathered.append((gw[:, c0 : c0 + P], gs[:, c0 : c0 + P]))
 
-        for e in range(E):
+        def first_layer(e):
+            if e in PERMUTED:
+                pw = keep.tile([P, 2 * H], U8, name=f"pw{e}", align_bytes=64)
+                ps = keep.tile([P, H], U8, name=f"ps{e}", align_bytes=64)
+                h_cols[e] = keep.tile([P, 4 * C], BF16, name=f"ht{e}", align_bytes=64)
+            else:
+                h_rows[e] = keep.tile([P, 2, H], BF16, name=f"hb{e}", align_bytes=64)
+            for b in range(2):
+                if 2 * e + b in starts:
+                    gather(2 * e + b)
+                words, scales = gathered[2 * e + b]
+                acc = psum_a.tile([P, H], F32, name="bank_a")
+                if e in PERMUTED:
+                    if b == 0:
+                        nc.vector.tensor_copy(
+                            pw[:].rearrange("p (t m d) -> p t m d", t=4, d=2),
+                            w1w[e].rearrange("p (m t d) -> p t m d", t=4, d=2),
+                        )
+                        nc.vector.tensor_copy(
+                            ps[:].rearrange("p (t m) -> p t m", t=4), w1s[e].rearrange("p (m t) -> p t m", t=4)
+                        )
+                    for t in range(4):
+                        nc.tensor.matmul_mx(
+                            out=acc[:, t * P : (t + 1) * P],
+                            lhsT=pw[:, 2 * t * P : 2 * (t + 1) * P].bitcast(FP4X4),
+                            lhsT_scale=ps[:, t * P : (t + 1) * P],
+                            rhs=words.bitcast(FP8X4),
+                            rhs_scale=scales,
+                            start=True,
+                            stop=True,
+                        )
+                    nc.scalar.activation(
+                        h_cols[e][:, b * H : (b + 1) * H].rearrange("p (s t) -> p s t", t=4),
+                        acc[:].rearrange("p (t s) -> p s t", t=4),
+                        RELU,
+                    )
+                    continue
+                nc.tensor.matmul_mx(
+                    out=acc[:],
+                    lhsT=words.bitcast(FP8X4),
+                    lhsT_scale=scales,
+                    rhs=w1w[e].bitcast(FP4X4),
+                    rhs_scale=w1s[e],
+                    start=True,
+                    stop=True,
+                )
+                nc.scalar.activation(
+                    h_rows[e][:, b, :].rearrange("s (u p d) -> s u p d", u=2, d=2),
+                    acc[:].rearrange("s (p u d) -> s u p d", u=2, d=2),
+                    RELU,
+                )
+
+        def turn(e):
+            if e in PERMUTED:
+                return
             words = h_rows[e][:].rearrange("s b i -> s (b i)").bitcast(F32)
-            turned = psum_t.tile([P, 4, P], F32, name="turned")
+            turned = psum_t.tile([P, 4, P], F32, name="bank_t")
             for j in range(4):
                 nc.tensor.transpose(turned[:, j, :], words[:, j * P : (j + 1) * P], ident[:])
-            ht = keep.tile([P, 4 * C], BF16, name=f"ht{e}", align_bytes=64)
-            dst = ht[:].bitcast(F32).rearrange("p (b s u) -> p b s u", b=2, u=2)
+            h_cols[e] = keep.tile([P, 4 * C], BF16, name=f"ht{e}", align_bytes=64)
+            dst = h_cols[e][:].bitcast(F32).rearrange("p (b s u) -> p b s u", b=2, u=2)
             src = turned[:].rearrange("p (b u) s -> p b s u", u=2)
             if e in VECTOR_TURNS:
                 nc.vector.tensor_copy(dst, src)
             else:
                 nc.scalar.copy(dst, src)
-            nc.vector.quantize_mx(out=hq[e][:].bitcast(FP8X4), scales=hs[e][:], in_=ht[:])
-            second_layer(e, 0)
-        for e in range(E):
-            second_layer(e, 1)
+
+        def second_layer(run, h):
+            acc = psum_y.tile([P, len(run) * C], F32, name="bank_y")
+            for j, e in enumerate(run):
+                nc.tensor.matmul_mx(
+                    out=acc[:, j * C : (j + 1) * C],
+                    lhsT=w2_tiles[0][e][:, 2 * h * P : 2 * (h + 1) * P].bitcast(FP4X4),
+                    lhsT_scale=w2s[:, e * N + h * P : e * N + (h + 1) * P],
+                    rhs=hq[e][:].bitcast(FP8X4),
+                    rhs_scale=hs[e][:],
+                    start=True,
+                    stop=True,
+                )
+            dst = y[h][:, run[0] * C : (run[-1] + 1) * C]
+            if h == 0 and run[0] in VECTOR_Y:
+                nc.vector.tensor_copy(dst, acc[:])
+            else:
+                nc.scalar.copy(dst, acc[:])
+
+        for step in range(E + LAG_T + LAG_Q + LAG_Y + 1):
+            if step < E:
+                first_layer(step)
+            if 0 <= step - LAG_T < E:
+                turn(step - LAG_T)
+            e = step - LAG_T - LAG_Q
+            if 0 <= e < E:
+                nc.vector.quantize_mx(out=hq[e][:].bitcast(FP8X4), scales=hs[e][:], in_=h_cols[e][:])
+            for run in Y_RUNS[0]:
+                if run[-1] == e - LAG_Y:
+                    second_layer(run, 0)
+        for run in Y_RUNS[1]:
+            second_layer(run, 1)
 
         for h, t0, t1 in TAIL:
+            width = t1 - t0
             prods = []
             for r in range(TOP):
-                prod = keep.tile([P, t1 - t0], F32, name=f"prod{h}_{t0}_{r}")
+                prod = keep.tile([P, width], F32, name=f"prod{h}_{t0}_{r}")
                 nc.vector.tensor_tensor(
-                    prod[:], y[h][:].indirect(pos_sb[r][:, t0 // 16 : t1 // 16]), gate_sb[h][r][:, t0:t1], MULT
+                    prod[:], y[h][:].indirect(pos_sb[r][:, t0 // 16 : t1 // 16]), gate_sb[h * TOP + r][:, t0:t1], MULT
                 )
                 prods.append(prod)
             rows = out[h * P : (h + 1) * P, t0:t1]
@@ -163,8 +231,7 @@ def tile_moe_pkd_mlp_relu_kernel(
                 nc.vector.tensor_tensor(prods[2][:], prods[0][:], prods[2][:], ADD)
                 nc.sync.dma_start(out=rows, in_=prods[2][:])
                 continue
-            width = t1 - t0
-            summed = psum_a.tile([P, width], F32, name="acc")
+            summed = psum_y.tile([P, width], F32, name="bank_y")
             for c0 in range(0, width, P):
                 for r in range(TOP):
                     nc.tensor.matmul(
@@ -177,9 +244,9 @@ def tile_moe_pkd_mlp_relu_kernel(
                     )
             by_token = keep.tile([P, width], F32, name=f"by_token{h}_{t0}")
             nc.scalar.copy(by_token[:], summed[:])
-            back = psum_a.tile([P, width], F32, name="acc")
+            back = psum_a.tile([P, width], F32, name="bank_a")
             for c0 in range(0, width, P):
                 nc.tensor.transpose(back[:, c0 : c0 + P], by_token[:, c0 : c0 + P], ident[:])
             result = keep.tile([P, width], F32, name=f"result{h}_{t0}")
             nc.scalar.copy(result[:], back[:])
-            nc.sync.dma_start(out=rows, in_=result[:])
+            nc.scalar.dma_start(out=rows, in_=result[:])

@@ -22,13 +22,13 @@ MULT = mybir.AluOpType.mult
 ADD = mybir.AluOpType.add
 
 GATHER_BLOCKS = (1, 3, 2, 4, 4, 4)
-VECTOR_TURNS = (4, 5, 6)
-PERMUTED = ()
+VECTOR_TURNS = (4, 5)
+PERMUTED = (6, 7, 8)
 Y_RUNS = (((0, 1), (2, 3), (4, 5), (6, 7), (8,)), ((0, 1), (2, 3), (4, 5), (6, 7), (8,)))
-VECTOR_Y = (0, 2)
+VECTOR_Y = (6,)
 TAIL = ((0, 0, 384), (0, 384, 768), (1, 0, 256), (1, 256, 512), (1, 512, 768))
 EARLY = 3
-LAG_T, LAG_Q, LAG_Y = 3, 0, 0
+LAG_T, LAG_Q, LAG_Y = 2, 0, 0
 
 
 def tile_moe_pkd_mlp_relu_kernel(
@@ -38,8 +38,8 @@ def tile_moe_pkd_mlp_relu_kernel(
     with ExitStack() as ctx:
         keep = ctx.enter_context(tc.tile_pool(name="keep", bufs=1))
         psum_a = ctx.enter_context(tc.psum_pool(name="psum_a", bufs=3))
-        psum_t = ctx.enter_context(tc.psum_pool(name="psum_t", bufs=3))
-        psum_y = ctx.enter_context(tc.psum_pool(name="psum_y", bufs=2))
+        psum_t = ctx.enter_context(tc.psum_pool(name="psum_t", bufs=2))
+        psum_y = ctx.enter_context(tc.psum_pool(name="psum_y", bufs=3))
 
         offs_sb = keep.tile([P, S // 16], U16, name="offs_sb")
         pos_sb = [keep.tile([P, T // 16], U16, name=f"pos_sb{r}") for r in range(TOP)]
@@ -86,14 +86,13 @@ def tile_moe_pkd_mlp_relu_kernel(
         w1w = load_words(w1_words, 2 * H, 0, 1, "w1w_a")
         nc.scalar.activation(warm[:, 4:5], warm[:, 0:1], RELU)
         load_scales((nc.sync, nc.sync, nc.sync, nc.sync), w1s_early, w1_scales[:, 0], H, 0, EARLY)
-        w1w += load_words(w1_words, 2 * H, 1, 3, "w1w_b")
+        w1w += load_words(w1_words, 2 * H, 1, 3, "w1w_b", "w1_b")
         load_scales((nc.sync,) * 4, w1s_late, w1_scales[:, 0], H, EARLY, E)
-        w1w += load_words(w1_words, 2 * H, 3, 6, "w1w_c")
-        w1w += load_words(w1_words, 2 * H, 6, 9, "w1w_d")
+        w1w_last = load_words(w1_words, 2 * H, 6, 9, "w1w_d")
+        w1w += load_words(w1_words, 2 * H, 3, 6, "w1w_c") + w1w_last
         load_scales((nc.sync,) * 4, w2s, w2_scales[:, 0], N, 0, E)
         for r, pos in enumerate((pos1, pos2, pos3)):
             nc.sync.dma_start(pos_sb[r][:], pos)
-        w2w = load_words(w2_words, 2 * N, 0, E, "w2w")
         for j in range(2 * TOP):
             h, r = divmod(j, TOP)
             nc.sync.dma_start(out=gate_sb[j][:], in_=gate[r, h * P : (h + 1) * P, :])
@@ -101,7 +100,7 @@ def tile_moe_pkd_mlp_relu_kernel(
         starts = {sum(GATHER_BLOCKS[:g]): g for g in range(len(GATHER_BLOCKS))}
         gathered = []
         h_rows, h_cols = {}, {}
-        w2_tiles = [w2w]
+        w2_tiles = []
         y = [keep.tile([P, S], F32, name=f"y{h}") for h in range(2)]
         hq = [keep.tile([P, C], U32, name=f"hq{e}", align_bytes=64) for e in range(E)]
         hs = [keep.tile([P, C], U8, name=f"hs{e}", align_bytes=64) for e in range(E)]
@@ -131,11 +130,11 @@ def tile_moe_pkd_mlp_relu_kernel(
                 acc = psum_a.tile([P, H], F32, name="bank_a")
                 if e in PERMUTED:
                     if b == 0:
-                        nc.vector.tensor_copy(
+                        nc.gpsimd.tensor_copy(
                             pw[:].rearrange("p (t m d) -> p t m d", t=4, d=2),
                             w1w[e].rearrange("p (m t d) -> p t m d", t=4, d=2),
                         )
-                        nc.vector.tensor_copy(
+                        nc.gpsimd.tensor_copy(
                             ps[:].rearrange("p (t m) -> p t m", t=4), w1s[e].rearrange("p (m t) -> p t m", t=4)
                         )
                     for t in range(4):
@@ -168,6 +167,8 @@ def tile_moe_pkd_mlp_relu_kernel(
                     acc[:].rearrange("s (p u d) -> s u p d", u=2, d=2),
                     RELU,
                 )
+            if e == 2:
+                w2_tiles.append(load_words(w2_words, 2 * N, 0, E, "w2w", "w1_b"))
 
         def turn(e):
             if e in PERMUTED:

@@ -7,6 +7,8 @@ K, T, E, C, H, N = 512, 768, 9, 256, 512, 256
 TOP = 3
 S = E * C
 P = 128
+PACK = 4
+LIST_ROWS = 16
 FLOPS = 2 * S * (K * H + H * N)
 
 F32 = mybir.dt.float32
@@ -21,14 +23,15 @@ RELU = mybir.ActivationFunctionType.Relu
 MULT = mybir.AluOpType.mult
 ADD = mybir.AluOpType.add
 
-GATHER_BLOCKS = (1, 3, 2, 4, 4, 4)
-VECTOR_TURNS = (4, 5)
-PERMUTED = (6, 7, 8)
-Y_RUNS = (((0, 1), (2, 3), (4, 5), (6, 7), (8,)), ((0, 1), (2, 3), (4, 5), (6, 7), (8,)))
-VECTOR_Y = (6,)
-TAIL = ((0, 0, 384), (0, 384, 768), (1, 0, 256), (1, 256, 512), (1, 512, 768))
-EARLY = 3
-LAG_T, LAG_Q, LAG_Y = 2, 0, 0
+GATHER_BLOCKS = (1, 3, 4, 4, 4, 2)
+TURNED = 3
+EARLY = 4
+PERMUTE_RUNS = ((3, 4), (4, 5), (5, 7), (7, 9))
+QUANTISE_RUNS = ((0, 4), (4, 6), (6, 8), (8, 9))
+SECOND_RUNS = (((0, 2), (2, 4), (4, 6), (6, 8), (8, 9)), ((0, 1), (1, 3), (3, 5), (5, 7), (7, 9)))
+VECTOR_TURN = 2
+VECTOR_SECOND = (0, 6)
+COMBINE_PIECES = ((0, 0, 384), (0, 384, 768), (1, 0, 384), (1, 384, 512), (1, 512, 768))
 
 
 def tile_moe_pkd_mlp_relu_kernel(
@@ -36,218 +39,218 @@ def tile_moe_pkd_mlp_relu_kernel(
 ):
     nc = tc.nc
     with ExitStack() as ctx:
-        keep = ctx.enter_context(tc.tile_pool(name="keep", bufs=1))
-        psum_a = ctx.enter_context(tc.psum_pool(name="psum_a", bufs=3))
-        psum_t = ctx.enter_context(tc.psum_pool(name="psum_t", bufs=2))
-        psum_y = ctx.enter_context(tc.psum_pool(name="psum_y", bufs=3))
+        sbuf = ctx.enter_context(tc.tile_pool(name="sbuf", bufs=1))
+        psum_first = ctx.enter_context(tc.psum_pool(name="psum_first", bufs=3))
+        psum_turn = ctx.enter_context(tc.psum_pool(name="psum_turn", bufs=2))
+        psum_rest = ctx.enter_context(tc.psum_pool(name="psum_rest", bufs=3))
 
-        offs_sb = keep.tile([P, S // 16], U16, name="offs_sb")
-        pos_sb = [keep.tile([P, T // 16], U16, name=f"pos_sb{r}") for r in range(TOP)]
-        xw = keep.tile([P, T], I32, name="xw", align_bytes=64)
-        xs = keep.tile([P, T], U8, name="xs", align_bytes=64)
-        w1s_early = keep.tile([P, EARLY * H], U8, name="w1s_early", align_bytes=64)
-        w1s_late = keep.tile([P, (E - EARLY) * H], U8, name="w1s_late", align_bytes=64)
-        w1s = [w1s_early[:, e * H : (e + 1) * H] for e in range(EARLY)]
-        w1s += [w1s_late[:, e * H : (e + 1) * H] for e in range(E - EARLY)]
-        w2s = keep.tile([P, E * N], U8, name="w2s", align_bytes=64)
-        gate_sb = [keep.tile([P, T], F32, name=f"gate{j}") for j in range(2 * TOP)]
-        ident = keep.tile([P, P], F32, name="ident")
-        warm = keep.tile([P, 8], F32, name="warm")
+        offs_sb = sbuf.tile([P, S // LIST_ROWS], U16, name="offs_sb")
+        pos_sb = [sbuf.tile([P, T // LIST_ROWS], U16, name=f"pos_sb{r}") for r in range(TOP)]
+        x_word_tile = sbuf.tile([P, T], I32, name="x_word_tile", align_bytes=64)
+        x_plane = sbuf.tile([P, T], U8, name="x_plane", align_bytes=64)
+        w1_plane_early = sbuf.tile([P, EARLY * H], U8, name="w1_plane_early", align_bytes=64)
+        w1_plane_late = sbuf.tile([P, (E - EARLY) * H], U8, name="w1_plane_late", align_bytes=64)
+        w2_plane = sbuf.tile([P, E * N], U8, name="w2_plane", align_bytes=64)
+        gate_sb = [[sbuf.tile([P, T], F32, name=f"gate{half}_{r}") for r in range(TOP)] for half in range(2)]
+        ident = sbuf.tile([P, P], F32, name="ident")
 
-        nc.vector.memset(w1s_early[:].bitcast(I32), 0)
-        nc.vector.memset(w1s_late[:].bitcast(I32), 0)
-        nc.vector.memset(w2s[:].bitcast(I32), 0)
-        nc.gpsimd.memset(warm[:], 0.0)
+        for plane in (w1_plane_early, w1_plane_late, w2_plane):
+            nc.vector.memset(plane[:].bitcast(I32), 0)
         make_identity(nc, ident[:])
 
-        def load_scales(queues, plane, scales, width, e0, e1):
+        def load_plane(plane, scales, first, end):
             for q in range(4):
-                queues[q].dma_start(
-                    out=plane[32 * q : 32 * q + 4, :].bitcast(I32).rearrange("r (e w) -> r e w", w=width // 4),
-                    in_=scales[e0:e1, 4 * q : 4 * q + 4, :].rearrange("e r w -> r e w").bitcast(I32),
+                nc.sync.dma_start(
+                    out=plane[32 * q : 32 * q + 4, :].bitcast(I32).rearrange("r (e w) -> r e w", e=end - first),
+                    in_=scales[first:end, 0, 4 * q : 4 * q + 4, :].rearrange("e r w -> r e w").bitcast(I32),
                 )
 
-        def load_words(words, width, e0, e1, name, tag=""):
-            tile = keep.tile([P, (e1 - e0) * width], U8, name=name, tag=tag, align_bytes=64)
+        def load_words(words, first, end, name):
+            tile = sbuf.tile([P, (end - first) * words.shape[-1]], U8, name=name, align_bytes=64)
             nc.sync.dma_start(
-                out=tile[:].bitcast(I32).rearrange("p (e w) -> p e w", w=width // 4),
-                in_=words[e0:e1, 0].rearrange("e p w -> p e w").bitcast(I32),
+                out=tile[:].bitcast(I32).rearrange("p (e w) -> p e w", e=end - first),
+                in_=words[first:end, 0].rearrange("e p w -> p e w").bitcast(I32),
             )
-            return [tile[:, j * width : (j + 1) * width] for j in range(e1 - e0)]
+            return tile
 
         nc.sync.dma_start(offs_sb[:], offs)
         for q in range(4):
             rows = x_scales[0, 4 * q : 4 * q + 4, :].bitcast(I32)
-            nc.scalar.dma_start(
-                out=xs[32 * q : 32 * q + 32, :].bitcast(I32),
+            (nc.sync if q < 2 else nc.scalar).dma_start(
+                out=x_plane[32 * q : 32 * q + 32, :].bitcast(I32),
                 in_=rows.unsqueeze(0).broadcast_to([8, 4, T // 4]),
             )
-        nc.sync.dma_start(out=xw[:], in_=x_words[0].rearrange("p t r -> p (t r)").bitcast(I32))
-        w1w = load_words(w1_words, 2 * H, 0, 1, "w1w_a")
-        nc.scalar.activation(warm[:, 4:5], warm[:, 0:1], RELU)
-        load_scales((nc.sync, nc.sync, nc.sync, nc.sync), w1s_early, w1_scales[:, 0], H, 0, EARLY)
-        w1w += load_words(w1_words, 2 * H, 1, 3, "w1w_b", "w1_b")
-        load_scales((nc.sync,) * 4, w1s_late, w1_scales[:, 0], H, EARLY, E)
-        w1w_last = load_words(w1_words, 2 * H, 6, 9, "w1w_d")
-        w1w += load_words(w1_words, 2 * H, 3, 6, "w1w_c") + w1w_last
-        load_scales((nc.sync,) * 4, w2s, w2_scales[:, 0], N, 0, E)
+        nc.sync.dma_start(out=x_word_tile[:], in_=x_words[0].rearrange("p t r -> p (t r)").bitcast(I32))
+        w1_first = load_words(w1_words, 0, 1, "w1_first")
+        load_plane(w1_plane_early, w1_scales, 0, EARLY)
+        w1_early = load_words(w1_words, 1, EARLY, "early_words")
+        load_plane(w1_plane_late, w1_scales, EARLY, E)
+        w1_late = load_words(w1_words, EARLY, E, "late_words")
+        load_plane(w2_plane, w2_scales, 0, E)
         for r, pos in enumerate((pos1, pos2, pos3)):
             nc.sync.dma_start(pos_sb[r][:], pos)
-        for j in range(2 * TOP):
-            h, r = divmod(j, TOP)
-            nc.sync.dma_start(out=gate_sb[j][:], in_=gate[r, h * P : (h + 1) * P, :])
+        for half in range(2):
+            for r in range(TOP):
+                nc.sync.dma_start(out=gate_sb[half][r][:], in_=gate[r, half * P : (half + 1) * P, :])
 
-        starts = {sum(GATHER_BLOCKS[:g]): g for g in range(len(GATHER_BLOCKS))}
-        gathered = []
-        h_rows, h_cols = {}, {}
-        w2_tiles = []
-        y = [keep.tile([P, S], F32, name=f"y{h}") for h in range(2)]
-        hq = [keep.tile([P, C], U32, name=f"hq{e}", align_bytes=64) for e in range(E)]
-        hs = [keep.tile([P, C], U8, name=f"hs{e}", align_bytes=64) for e in range(E)]
+        def w1_as_loaded(first, end):
+            words, base = (w1_late, EARLY) if first >= EARLY else (w1_early, 1) if first else (w1_first, 0)
+            plane, plane_base = (w1_plane_late, EARLY) if first >= EARLY else (w1_plane_early, 0)
+            return (
+                words[:, (first - base) * 2 * H : (end - base) * 2 * H],
+                plane[:, (first - plane_base) * H : (end - plane_base) * H],
+            )
 
-        def gather(block):
-            g = starts[block]
+        gather_at = {sum(GATHER_BLOCKS[:g]): g for g in range(len(GATHER_BLOCKS))}
+        permute_end = dict(PERMUTE_RUNS)
+        slot_tokens = []
+        w1_permuted = {}
+        h_by_slot = {}
+        h_by_i = sbuf.tile([P, PACK * S], BF16, name="h_by_i", align_bytes=64)
+
+        def gather_tokens(block):
+            g = gather_at[block]
             width = GATHER_BLOCKS[g] * P
-            picks = offs_sb[:, block * P // 16 : (block * P + width) // 16]
-            gw = keep.tile([P, width], U32, name=f"gw{g}", tag=f"gw{g % 2}", align_bytes=64)
-            gs = keep.tile([P, width], U8, name=f"gs{g}", tag=f"gs{g % 2}", align_bytes=64)
-            nc.vector.tensor_copy(gw[:], xw[:].bitcast(U32).indirect(picks))
-            nc.vector.tensor_copy(gs[:], xs[:].indirect(picks))
+            picks = offs_sb[:, block * P // LIST_ROWS : (block * P + width) // LIST_ROWS]
+            words = sbuf.tile([P, width], U32, name=f"slot_words{g % 2}", align_bytes=64)
+            scales = sbuf.tile([P, width], U8, name=f"slot_scales{g % 2}", align_bytes=64)
+            nc.vector.tensor_copy(words[:], x_word_tile[:].bitcast(U32).indirect(picks))
+            nc.vector.tensor_copy(scales[:], x_plane[:].indirect(picks))
             for c0 in range(0, width, P):
-                gathered.append((gw[:, c0 : c0 + P], gs[:, c0 : c0 + P]))
+                slot_tokens.append((words[:, c0 : c0 + P].bitcast(FP8X4), scales[:, c0 : c0 + P]))
+
+        def permute_w1(first):
+            end = permute_end[first]
+            raw_words, raw_scales = w1_as_loaded(first, end)
+            words = sbuf.tile([P, (end - first) * 2 * H], U8, name=f"permuted_words{first}", align_bytes=64)
+            scales = sbuf.tile([P, (end - first) * H], U8, name=f"permuted_scales{first}", align_bytes=64)
+            for dst, src in ((scales[:], raw_scales), (words[:].bitcast(U16), raw_words.bitcast(U16))):
+                nc.gpsimd.tensor_copy(
+                    dst.rearrange("p (e t m) -> p e t m", t=PACK, m=P),
+                    src.rearrange("p (e m t) -> p e t m", t=PACK, m=P),
+                )
+            for e in range(first, end):
+                j = e - first
+                w1_permuted[e] = (words[:, j * 2 * H : (j + 1) * 2 * H], scales[:, j * H : (j + 1) * H])
 
         def first_layer(e):
-            if e in PERMUTED:
-                pw = keep.tile([P, 2 * H], U8, name=f"pw{e}", align_bytes=64)
-                ps = keep.tile([P, H], U8, name=f"ps{e}", align_bytes=64)
-                h_cols[e] = keep.tile([P, 4 * C], BF16, name=f"ht{e}", align_bytes=64)
-            else:
-                h_rows[e] = keep.tile([P, 2, H], BF16, name=f"hb{e}", align_bytes=64)
+            if e < TURNED:
+                h_by_slot[e] = sbuf.tile([P, 2, H], BF16, name=f"h_by_slot{e}", align_bytes=64)
             for b in range(2):
-                if 2 * e + b in starts:
-                    gather(2 * e + b)
-                words, scales = gathered[2 * e + b]
-                acc = psum_a.tile([P, H], F32, name="bank_a")
-                if e in PERMUTED:
-                    if b == 0:
-                        nc.gpsimd.tensor_copy(
-                            pw[:].rearrange("p (t m d) -> p t m d", t=4, d=2),
-                            w1w[e].rearrange("p (m t d) -> p t m d", t=4, d=2),
-                        )
-                        nc.gpsimd.tensor_copy(
-                            ps[:].rearrange("p (t m) -> p t m", t=4), w1s[e].rearrange("p (m t) -> p t m", t=4)
-                        )
-                    for t in range(4):
+                block = 2 * e + b
+                if block in gather_at:
+                    gather_tokens(block)
+                if b == 0 and e in permute_end:
+                    permute_w1(e)
+                token_words, token_scales = slot_tokens[block]
+                acc = psum_first.tile([P, H], F32, name="first_bank")
+                if e < TURNED:
+                    words, scales = w1_as_loaded(e, e + 1)
+                    nc.tensor.matmul_mx(
+                        out=acc[:],
+                        lhsT=token_words,
+                        lhsT_scale=token_scales,
+                        rhs=words.bitcast(FP4X4),
+                        rhs_scale=scales,
+                        start=True,
+                        stop=True,
+                    )
+                    nc.scalar.activation(
+                        h_by_slot[e][:, b, :].rearrange("s (u p d) -> s u p d", u=2, d=2),
+                        acc[:].rearrange("s (p u d) -> s u p d", u=2, d=2),
+                        RELU,
+                    )
+                else:
+                    words, scales = w1_permuted[e]
+                    for t in range(PACK):
                         nc.tensor.matmul_mx(
                             out=acc[:, t * P : (t + 1) * P],
-                            lhsT=pw[:, 2 * t * P : 2 * (t + 1) * P].bitcast(FP4X4),
-                            lhsT_scale=ps[:, t * P : (t + 1) * P],
-                            rhs=words.bitcast(FP8X4),
-                            rhs_scale=scales,
+                            lhsT=words[:, 2 * t * P : 2 * (t + 1) * P].bitcast(FP4X4),
+                            lhsT_scale=scales[:, t * P : (t + 1) * P],
+                            rhs=token_words,
+                            rhs_scale=token_scales,
                             start=True,
                             stop=True,
                         )
                     nc.scalar.activation(
-                        h_cols[e][:, b * H : (b + 1) * H].rearrange("p (s t) -> p s t", t=4),
-                        acc[:].rearrange("p (t s) -> p s t", t=4),
+                        h_by_i[:, block * H : (block + 1) * H].rearrange("p (s t) -> p s t", t=PACK),
+                        acc[:].rearrange("p (t s) -> p s t", t=PACK),
                         RELU,
                     )
-                    continue
-                nc.tensor.matmul_mx(
-                    out=acc[:],
-                    lhsT=words.bitcast(FP8X4),
-                    lhsT_scale=scales,
-                    rhs=w1w[e].bitcast(FP4X4),
-                    rhs_scale=w1s[e],
-                    start=True,
-                    stop=True,
-                )
-                nc.scalar.activation(
-                    h_rows[e][:, b, :].rearrange("s (u p d) -> s u p d", u=2, d=2),
-                    acc[:].rearrange("s (p u d) -> s u p d", u=2, d=2),
-                    RELU,
-                )
-            if e == 2:
-                w2_tiles.append(load_words(w2_words, 2 * N, 0, E, "w2w", "w1_b"))
 
         def turn(e):
-            if e in PERMUTED:
-                return
-            words = h_rows[e][:].rearrange("s b i -> s (b i)").bitcast(F32)
-            turned = psum_t.tile([P, 4, P], F32, name="bank_t")
+            pairs = h_by_slot[e][:].rearrange("s b i -> s (b i)").bitcast(F32)
+            turned = psum_turn.tile([P, 4, P], F32, name="turn_bank")
             for j in range(4):
-                nc.tensor.transpose(turned[:, j, :], words[:, j * P : (j + 1) * P], ident[:])
-            h_cols[e] = keep.tile([P, 4 * C], BF16, name=f"ht{e}", align_bytes=64)
-            dst = h_cols[e][:].bitcast(F32).rearrange("p (b s u) -> p b s u", b=2, u=2)
+                nc.tensor.transpose(turned[:, j, :], pairs[:, j * P : (j + 1) * P], ident[:])
+            dst = h_by_i[:, e * PACK * C : (e + 1) * PACK * C].bitcast(F32).rearrange("p (b s u) -> p b s u", b=2, u=2)
             src = turned[:].rearrange("p (b u) s -> p b s u", u=2)
-            if e in VECTOR_TURNS:
-                nc.vector.tensor_copy(dst, src)
-            else:
-                nc.scalar.copy(dst, src)
+            (nc.vector.tensor_copy if e == VECTOR_TURN else nc.scalar.copy)(dst, src)
 
-        def second_layer(run, h):
-            acc = psum_y.tile([P, len(run) * C], F32, name="bank_y")
-            for j, e in enumerate(run):
-                nc.tensor.matmul_mx(
-                    out=acc[:, j * C : (j + 1) * C],
-                    lhsT=w2_tiles[0][e][:, 2 * h * P : 2 * (h + 1) * P].bitcast(FP4X4),
-                    lhsT_scale=w2s[:, e * N + h * P : e * N + (h + 1) * P],
-                    rhs=hq[e][:].bitcast(FP8X4),
-                    rhs_scale=hs[e][:],
-                    start=True,
-                    stop=True,
-                )
-            dst = y[h][:, run[0] * C : (run[-1] + 1) * C]
-            if h == 0 and run[0] in VECTOR_Y:
-                nc.vector.tensor_copy(dst, acc[:])
-            else:
-                nc.scalar.copy(dst, acc[:])
+        for e in range(E):
+            first_layer(e)
+            if e == EARLY - 1:
+                w2_tile = load_words(w2_words, 0, E, "early_words")
+            if 1 <= e <= TURNED:
+                turn(e - 1)
 
-        for step in range(E + LAG_T + LAG_Q + LAG_Y + 1):
-            if step < E:
-                first_layer(step)
-            if 0 <= step - LAG_T < E:
-                turn(step - LAG_T)
-            e = step - LAG_T - LAG_Q
-            if 0 <= e < E:
-                nc.vector.quantize_mx(out=hq[e][:].bitcast(FP8X4), scales=hs[e][:], in_=h_cols[e][:])
-            for run in Y_RUNS[0]:
-                if run[-1] == e - LAG_Y:
-                    second_layer(run, 0)
-        for run in Y_RUNS[1]:
-            second_layer(run, 1)
+        h_words = sbuf.tile([P, S], U32, name="late_words", align_bytes=64)
+        h_plane = sbuf.tile([P, S], U8, name="h_plane", align_bytes=64)
+        for first, end in QUANTISE_RUNS:
+            nc.vector.quantize_mx(
+                out=h_words[:, first * C : end * C].bitcast(FP8X4),
+                scales=h_plane[:, first * C : end * C],
+                in_=h_by_i[:, first * PACK * C : end * PACK * C],
+            )
 
-        for h, t0, t1 in TAIL:
+        y = [sbuf.tile([P, S], F32, name=f"y{half}") for half in range(2)]
+        for half in range(2):
+            for first, end in SECOND_RUNS[half]:
+                acc = psum_rest.tile([P, (end - first) * C], F32, name="rest_bank")
+                for e in range(first, end):
+                    col = e * N + half * P
+                    nc.tensor.matmul_mx(
+                        out=acc[:, (e - first) * C : (e - first + 1) * C],
+                        lhsT=w2_tile[:, 2 * col : 2 * (col + P)].bitcast(FP4X4),
+                        lhsT_scale=w2_plane[:, col : col + P],
+                        rhs=h_words[:, e * C : (e + 1) * C].bitcast(FP8X4),
+                        rhs_scale=h_plane[:, e * C : (e + 1) * C],
+                        start=True,
+                        stop=True,
+                    )
+                copy = nc.vector.tensor_copy if (half, first) == VECTOR_SECOND else nc.scalar.copy
+                copy(y[half][:, first * C : end * C], acc[:])
+
+        for half, t0, t1 in COMBINE_PIECES:
             width = t1 - t0
-            prods = []
+            products = []
             for r in range(TOP):
-                prod = keep.tile([P, width], F32, name=f"prod{h}_{t0}_{r}")
-                nc.vector.tensor_tensor(
-                    prod[:], y[h][:].indirect(pos_sb[r][:, t0 // 16 : t1 // 16]), gate_sb[h * TOP + r][:, t0:t1], MULT
-                )
-                prods.append(prod)
-            rows = out[h * P : (h + 1) * P, t0:t1]
-            if (h, t0, t1) == TAIL[-1]:
-                nc.vector.tensor_tensor(prods[0][:], prods[0][:], prods[1][:], ADD)
-                nc.vector.tensor_tensor(prods[2][:], prods[0][:], prods[2][:], ADD)
-                nc.sync.dma_start(out=rows, in_=prods[2][:])
+                product = sbuf.tile([P, width], F32, name=f"product{half}_{t0}_{r}")
+                picks = pos_sb[r][:, t0 // LIST_ROWS : t1 // LIST_ROWS]
+                nc.vector.tensor_tensor(product[:], y[half][:].indirect(picks), gate_sb[half][r][:, t0:t1], MULT)
+                products.append(product)
+            out_piece = out[half * P : (half + 1) * P, t0:t1]
+            if (half, t0, t1) == COMBINE_PIECES[-1]:
+                nc.vector.tensor_tensor(products[0][:], products[0][:], products[1][:], ADD)
+                nc.vector.tensor_tensor(products[2][:], products[0][:], products[2][:], ADD)
+                nc.sync.dma_start(out=out_piece, in_=products[2][:])
                 continue
-            summed = psum_y.tile([P, width], F32, name="bank_y")
+            summed = psum_rest.tile([P, width], F32, name="rest_bank")
             for c0 in range(0, width, P):
                 for r in range(TOP):
                     nc.tensor.matmul(
                         summed[:, c0 : c0 + P],
-                        lhsT=prods[r][:, c0 : c0 + P],
+                        lhsT=products[r][:, c0 : c0 + P],
                         rhs=ident[:],
                         is_transpose=True,
                         start=(r == 0),
                         stop=(r == TOP - 1),
                     )
-            by_token = keep.tile([P, width], F32, name=f"by_token{h}_{t0}")
+            by_token = sbuf.tile([P, width], F32, name=f"by_token{half}_{t0}")
             nc.scalar.copy(by_token[:], summed[:])
-            back = psum_a.tile([P, width], F32, name="bank_a")
+            back = psum_rest.tile([P, width], F32, name="rest_bank")
             for c0 in range(0, width, P):
                 nc.tensor.transpose(back[:, c0 : c0 + P], by_token[:, c0 : c0 + P], ident[:])
-            result = keep.tile([P, width], F32, name=f"result{h}_{t0}")
+            result = sbuf.tile([P, width], F32, name=f"result{half}_{t0}")
             nc.scalar.copy(result[:], back[:])
-            nc.scalar.dma_start(out=rows, in_=result[:])
+            nc.scalar.dma_start(out=out_piece, in_=result[:])

@@ -23,13 +23,13 @@ RELU = mybir.ActivationFunctionType.Relu
 MULT = mybir.AluOpType.mult
 ADD = mybir.AluOpType.add
 
-GATHER_BLOCKS = (1, 3, 4, 4, 4, 2)
-TURNED = 3
+GATHER_BLOCKS = (1, 3, 2, 4, 4, 4)
+TURNED = 5
 EARLY = 4
-PERMUTE_RUNS = ((3, 4), (4, 5), (5, 7), (7, 9))
-QUANTISE_RUNS = ((0, 4), (4, 6), (6, 8), (8, 9))
+PERMUTE_RUNS = ((5, 7), (7, 9))
+QUANTISE_RUNS = ((0, 2), (2, 4), (4, 6), (6, 8), (8, 9))
 SECOND_RUNS = (((0, 2), (2, 4), (4, 6), (6, 8), (8, 9)), ((0, 1), (1, 3), (3, 5), (5, 7), (7, 9)))
-VECTOR_TURN = 2
+VECTOR_TURNS = (3, 4)
 VECTOR_SECOND = (0, 6)
 COMBINE_PIECES = ((0, 0, 384), (0, 384, 768), (1, 0, 384), (1, 384, 512), (1, 512, 768))
 
@@ -185,7 +185,7 @@ def tile_moe_pkd_mlp_relu_kernel(
                 nc.tensor.transpose(turned[:, j, :], pairs[:, j * P : (j + 1) * P], ident[:])
             dst = h_by_i[:, e * PACK * C : (e + 1) * PACK * C].bitcast(F32).rearrange("p (b s u) -> p b s u", b=2, u=2)
             src = turned[:].rearrange("p (b u) s -> p b s u", u=2)
-            (nc.vector.tensor_copy if e == VECTOR_TURN else nc.scalar.copy)(dst, src)
+            (nc.vector.tensor_copy if e in VECTOR_TURNS else nc.scalar.copy)(dst, src)
 
         for e in range(E):
             first_layer(e)

@@ -23,15 +23,20 @@ RELU = mybir.ActivationFunctionType.Relu
 MULT = mybir.AluOpType.mult
 ADD = mybir.AluOpType.add
 
-GATHER_BLOCKS = (1, 3, 2, 4, 4, 4)
-TURNED = 5
+WORD_GATHERS = ((1, 0), (1, 1), (2, 2), (3, 3), (4, 1), (4, 2), (3, 3))
+BYTE_GATHERS = ((2, 1), (2, 2), (4, 1), (4, 2), (3, 1), (3, 2))
+TURNED = 2
 EARLY = 4
-PERMUTE_RUNS = ((5, 7), (7, 9))
+PERMUTE_RUNS = ((2, 3), (3, 4), (4, 5), (5, 7), (7, 8), (8, 9))
 QUANTISE_RUNS = ((0, 2), (2, 4), (4, 6), (6, 8), (8, 9))
-SECOND_RUNS = (((0, 2), (2, 4), (4, 6), (6, 8), (8, 9)), ((0, 1), (1, 3), (3, 5), (5, 7), (7, 9)))
-VECTOR_TURNS = (3, 4)
-VECTOR_SECOND = (0, 6)
+SECOND_RUNS = ((0, 2), (2, 4), (4, 6), (6, 8), (8, 9))
+FIRST_BANKS = 6
+SECOND_BANKS = ((2, 3, 4, 5, 0), (5, 0, 5, 0, 5))
+VECTOR_BLOCKS = (13,)
+VECTOR_SECOND = ((0, 0), (0, 4), (0, 8))
 COMBINE_PIECES = ((0, 0, 384), (0, 384, 768), (1, 0, 384), (1, 384, 512), (1, 512, 768))
+SUM_BANKS = (5, 5, 4, 1)
+BACK_BANKS = (2, 3)
 
 
 def tile_moe_pkd_mlp_relu_kernel(
@@ -40,9 +45,10 @@ def tile_moe_pkd_mlp_relu_kernel(
     nc = tc.nc
     with ExitStack() as ctx:
         sbuf = ctx.enter_context(tc.tile_pool(name="sbuf", bufs=1))
-        psum_first = ctx.enter_context(tc.psum_pool(name="psum_first", bufs=3))
-        psum_turn = ctx.enter_context(tc.psum_pool(name="psum_turn", bufs=2))
-        psum_rest = ctx.enter_context(tc.psum_pool(name="psum_rest", bufs=3))
+        psum = ctx.enter_context(tc.psum_pool(name="psum", bufs=1))
+
+        def bank(number, width):
+            return psum.tile([P, width], F32, name=f"bank{number}")
 
         offs_sb = sbuf.tile([P, S // LIST_ROWS], U16, name="offs_sb")
         pos_sb = [sbuf.tile([P, T // LIST_ROWS], U16, name=f"pos_sb{r}") for r in range(TOP)]
@@ -51,11 +57,11 @@ def tile_moe_pkd_mlp_relu_kernel(
         w1_plane_early = sbuf.tile([P, EARLY * H], U8, name="w1_plane_early", align_bytes=64)
         w1_plane_late = sbuf.tile([P, (E - EARLY) * H], U8, name="w1_plane_late", align_bytes=64)
         w2_plane = sbuf.tile([P, E * N], U8, name="w2_plane", align_bytes=64)
-        gate_sb = [[sbuf.tile([P, T], F32, name=f"gate{half}_{r}") for r in range(TOP)] for half in range(2)]
+        gate_sb = sbuf.tile([P, TOP, T], F32, name="gate_sb")
         ident = sbuf.tile([P, P], F32, name="ident")
 
         for plane in (w1_plane_early, w1_plane_late, w2_plane):
-            nc.vector.memset(plane[:].bitcast(I32), 0)
+            nc.gpsimd.memset(plane[:].bitcast(I32), 0)
         make_identity(nc, ident[:])
 
         def load_plane(plane, scales, first, end):
@@ -81,47 +87,42 @@ def tile_moe_pkd_mlp_relu_kernel(
                 in_=rows.unsqueeze(0).broadcast_to([8, 4, T // 4]),
             )
         nc.sync.dma_start(out=x_word_tile[:], in_=x_words[0].rearrange("p t r -> p (t r)").bitcast(I32))
-        w1_first = load_words(w1_words, 0, 1, "w1_first")
+        w1_first = load_words(w1_words, 0, TURNED, "w1_first")
         load_plane(w1_plane_early, w1_scales, 0, EARLY)
-        w1_early = load_words(w1_words, 1, EARLY, "early_words")
+        w1_early = load_words(w1_words, TURNED, EARLY, "w1_early")
         load_plane(w1_plane_late, w1_scales, EARLY, E)
-        w1_late = load_words(w1_words, EARLY, E, "late_words")
+        w1_late = load_words(w1_words, EARLY, E, "w1_late")
         load_plane(w2_plane, w2_scales, 0, E)
+        w2_tile = load_words(w2_words, 0, E, "w2_tile")
         for r, pos in enumerate((pos1, pos2, pos3)):
             nc.sync.dma_start(pos_sb[r][:], pos)
-        for half in range(2):
-            for r in range(TOP):
-                nc.sync.dma_start(out=gate_sb[half][r][:], in_=gate[r, half * P : (half + 1) * P, :])
+        nc.sync.dma_start(out=gate_sb[:], in_=gate[:, 0:P, :].rearrange("r p t -> p r t"))
 
-        def w1_as_loaded(first, end):
-            words, base = (w1_late, EARLY) if first >= EARLY else (w1_early, 1) if first else (w1_first, 0)
-            plane, plane_base = (w1_plane_late, EARLY) if first >= EARLY else (w1_plane_early, 0)
-            return (
-                words[:, (first - base) * 2 * H : (end - base) * 2 * H],
-                plane[:, (first - plane_base) * H : (end - plane_base) * H],
-            )
+        def gather(window, dtype, runs, name):
+            blocks = []
+            for count, buffer in runs:
+                start, width = len(blocks) * P, count * P
+                picks = offs_sb[:, start // LIST_ROWS : (start + width) // LIST_ROWS]
+                tile = sbuf.tile([P, width], dtype, name=f"{name}{buffer}", align_bytes=64)
+                blocks.extend((tile, window, picks if c0 == 0 else None, c0) for c0 in range(0, width, P))
+            return blocks
 
-        gather_at = {sum(GATHER_BLOCKS[:g]): g for g in range(len(GATHER_BLOCKS))}
-        permute_end = dict(PERMUTE_RUNS)
-        slot_tokens = []
+        word_blocks = gather(x_word_tile[:].bitcast(U32), U32, WORD_GATHERS, "slot_words")
+        byte_blocks = gather(x_plane[:], U8, BYTE_GATHERS, "slot_scales")
+
+        def slot_tokens(block):
+            for tile, window, picks, c0 in (byte_blocks[block], word_blocks[block]):
+                if picks is not None:
+                    nc.vector.tensor_copy(tile[:], window.indirect(picks))
+            words, scales = word_blocks[block], byte_blocks[block]
+            return words[0][:, words[3] : words[3] + P].bitcast(FP8X4), scales[0][:, scales[3] : scales[3] + P]
+
         w1_permuted = {}
-        h_by_slot = {}
-        h_by_i = sbuf.tile([P, PACK * S], BF16, name="h_by_i", align_bytes=64)
-
-        def gather_tokens(block):
-            g = gather_at[block]
-            width = GATHER_BLOCKS[g] * P
-            picks = offs_sb[:, block * P // LIST_ROWS : (block * P + width) // LIST_ROWS]
-            words = sbuf.tile([P, width], U32, name=f"slot_words{g % 2}", align_bytes=64)
-            scales = sbuf.tile([P, width], U8, name=f"slot_scales{g % 2}", align_bytes=64)
-            nc.vector.tensor_copy(words[:], x_word_tile[:].bitcast(U32).indirect(picks))
-            nc.vector.tensor_copy(scales[:], x_plane[:].indirect(picks))
-            for c0 in range(0, width, P):
-                slot_tokens.append((words[:, c0 : c0 + P].bitcast(FP8X4), scales[:, c0 : c0 + P]))
-
-        def permute_w1(first):
-            end = permute_end[first]
-            raw_words, raw_scales = w1_as_loaded(first, end)
+        for first, end in PERMUTE_RUNS:
+            loaded, base = (w1_early, TURNED) if first < EARLY else (w1_late, EARLY)
+            raw_words = loaded[:, (first - base) * 2 * H : (end - base) * 2 * H]
+            plane, base = (w1_plane_early, 0) if first < EARLY else (w1_plane_late, EARLY)
+            raw_scales = plane[:, (first - base) * H : (end - base) * H]
             words = sbuf.tile([P, (end - first) * 2 * H], U8, name=f"permuted_words{first}", align_bytes=64)
             scales = sbuf.tile([P, (end - first) * H], U8, name=f"permuted_scales{first}", align_bytes=64)
             for dst, src in ((scales[:], raw_scales), (words[:].bitcast(U16), raw_words.bitcast(U16))):
@@ -133,25 +134,23 @@ def tile_moe_pkd_mlp_relu_kernel(
                 j = e - first
                 w1_permuted[e] = (words[:, j * 2 * H : (j + 1) * 2 * H], scales[:, j * H : (j + 1) * H])
 
+        h_by_slot = {}
+        h_by_i = sbuf.tile([P, PACK * S], BF16, name="h_by_i", align_bytes=64)
+
         def first_layer(e):
             if e < TURNED:
                 h_by_slot[e] = sbuf.tile([P, 2, H], BF16, name=f"h_by_slot{e}", align_bytes=64)
             for b in range(2):
                 block = 2 * e + b
-                if block in gather_at:
-                    gather_tokens(block)
-                if b == 0 and e in permute_end:
-                    permute_w1(e)
-                token_words, token_scales = slot_tokens[block]
-                acc = psum_first.tile([P, H], F32, name="first_bank")
+                token_words, token_scales = slot_tokens(block)
+                acc = bank(block % FIRST_BANKS, H)
                 if e < TURNED:
-                    words, scales = w1_as_loaded(e, e + 1)
                     nc.tensor.matmul_mx(
                         out=acc[:],
                         lhsT=token_words,
                         lhsT_scale=token_scales,
-                        rhs=words.bitcast(FP4X4),
-                        rhs_scale=scales,
+                        rhs=w1_first[:, e * 2 * H : (e + 1) * 2 * H].bitcast(FP4X4),
+                        rhs_scale=w1_plane_early[:, e * H : (e + 1) * H],
                         start=True,
                         stop=True,
                     )
@@ -172,30 +171,28 @@ def tile_moe_pkd_mlp_relu_kernel(
                             start=True,
                             stop=True,
                         )
-                    nc.scalar.activation(
-                        h_by_i[:, block * H : (block + 1) * H].rearrange("p (s t) -> p s t", t=PACK),
-                        acc[:].rearrange("p (t s) -> p s t", t=PACK),
-                        RELU,
-                    )
+                    dst = h_by_i[:, block * H : (block + 1) * H].rearrange("p (s t) -> p s t", t=PACK)
+                    src = acc[:].rearrange("p (t s) -> p s t", t=PACK)
+                    if block in VECTOR_BLOCKS:
+                        nc.vector.tensor_scalar_max(dst, src, 0.0)
+                    else:
+                        nc.scalar.activation(dst, src, RELU)
 
         def turn(e):
             pairs = h_by_slot[e][:].rearrange("s b i -> s (b i)").bitcast(F32)
-            turned = psum_turn.tile([P, 4, P], F32, name="turn_bank")
+            turned = bank(FIRST_BANKS + e % 2, 4 * P)
             for j in range(4):
-                nc.tensor.transpose(turned[:, j, :], pairs[:, j * P : (j + 1) * P], ident[:])
+                nc.tensor.transpose(turned[:, j * P : (j + 1) * P], pairs[:, j * P : (j + 1) * P], ident[:])
             dst = h_by_i[:, e * PACK * C : (e + 1) * PACK * C].bitcast(F32).rearrange("p (b s u) -> p b s u", b=2, u=2)
-            src = turned[:].rearrange("p (b u) s -> p b s u", u=2)
-            (nc.vector.tensor_copy if e in VECTOR_TURNS else nc.scalar.copy)(dst, src)
+            nc.scalar.copy(dst, turned[:].rearrange("p (b u s) -> p b s u", b=2, u=2))
 
         for e in range(E):
             first_layer(e)
-            if e == EARLY - 1:
-                w2_tile = load_words(w2_words, 0, E, "early_words")
             if 1 <= e <= TURNED:
                 turn(e - 1)
 
-        h_words = sbuf.tile([P, S], U32, name="late_words", align_bytes=64)
-        h_plane = sbuf.tile([P, S], U8, name="h_plane", align_bytes=64)
+        h_words = sbuf.tile([P, S], U32, name="x_word_tile", align_bytes=64)
+        h_plane = sbuf.tile([P, S], U8, name="x_plane", align_bytes=64)
         for first, end in QUANTISE_RUNS:
             nc.vector.quantize_mx(
                 out=h_words[:, first * C : end * C].bitcast(FP8X4),
@@ -205,8 +202,8 @@ def tile_moe_pkd_mlp_relu_kernel(
 
         y = [sbuf.tile([P, S], F32, name=f"y{half}") for half in range(2)]
         for half in range(2):
-            for first, end in SECOND_RUNS[half]:
-                acc = psum_rest.tile([P, (end - first) * C], F32, name="rest_bank")
+            for (first, end), number in zip(SECOND_RUNS, SECOND_BANKS[half]):
+                acc = bank(number, (end - first) * C)
                 for e in range(first, end):
                     col = e * N + half * P
                     nc.tensor.matmul_mx(
@@ -218,16 +215,16 @@ def tile_moe_pkd_mlp_relu_kernel(
                         start=True,
                         stop=True,
                     )
-                copy = nc.vector.tensor_copy if (half, first) == VECTOR_SECOND else nc.scalar.copy
+                copy = nc.vector.tensor_copy if (half, first) in VECTOR_SECOND else nc.scalar.copy
                 copy(y[half][:, first * C : end * C], acc[:])
 
-        for half, t0, t1 in COMBINE_PIECES:
+        for piece, (half, t0, t1) in enumerate(COMBINE_PIECES):
             width = t1 - t0
             products = []
             for r in range(TOP):
                 product = sbuf.tile([P, width], F32, name=f"product{half}_{t0}_{r}")
                 picks = pos_sb[r][:, t0 // LIST_ROWS : t1 // LIST_ROWS]
-                nc.vector.tensor_tensor(product[:], y[half][:].indirect(picks), gate_sb[half][r][:, t0:t1], MULT)
+                nc.vector.tensor_tensor(product[:], y[half][:].indirect(picks), gate_sb[:, r, t0:t1], MULT)
                 products.append(product)
             out_piece = out[half * P : (half + 1) * P, t0:t1]
             if (half, t0, t1) == COMBINE_PIECES[-1]:
@@ -235,7 +232,7 @@ def tile_moe_pkd_mlp_relu_kernel(
                 nc.vector.tensor_tensor(products[2][:], products[0][:], products[2][:], ADD)
                 nc.sync.dma_start(out=out_piece, in_=products[2][:])
                 continue
-            summed = psum_rest.tile([P, width], F32, name="rest_bank")
+            summed = bank(SUM_BANKS[piece], width)
             for c0 in range(0, width, P):
                 for r in range(TOP):
                     nc.tensor.matmul(
@@ -248,7 +245,7 @@ def tile_moe_pkd_mlp_relu_kernel(
                     )
             by_token = sbuf.tile([P, width], F32, name=f"by_token{half}_{t0}")
             nc.scalar.copy(by_token[:], summed[:])
-            back = psum_rest.tile([P, width], F32, name="rest_bank")
+            back = bank(BACK_BANKS[piece % 2], width)
             for c0 in range(0, width, P):
                 nc.tensor.transpose(back[:, c0 : c0 + P], by_token[:, c0 : c0 + P], ident[:])
             result = sbuf.tile([P, width], F32, name=f"result{half}_{t0}")

@@ -23,20 +23,26 @@ RELU = mybir.ActivationFunctionType.Relu
 MULT = mybir.AluOpType.mult
 ADD = mybir.AluOpType.add
 
-WORD_GATHERS = ((1, 0), (1, 1), (2, 2), (3, 3), (4, 1), (4, 2), (3, 3))
-BYTE_GATHERS = ((2, 1), (2, 2), (4, 1), (4, 2), (3, 1), (3, 2))
-TURNED = 2
+WORD_GATHERS = ((1, 0), (1, 1), (2, 2), (2, 3), (4, 1), (4, 2), (4, 3))
+BYTE_GATHERS = ((2, 4), (2, 5), (2, 0), (4, 4), (4, 5), (4, 0))
+TURNED = (0, 1, 2)
+FIRST = 2
+LATE = 6
+TURN_LAG = 2
+VECTOR_TURNS = ()
 EARLY = 4
-PERMUTE_RUNS = ((2, 3), (3, 4), (4, 5), (5, 7), (7, 8), (8, 9))
+PERMUTE_RUNS = ((3, 4), (4, 6), (6, 8), (8, 9))
 QUANTISE_RUNS = ((0, 2), (2, 4), (4, 6), (6, 8), (8, 9))
 SECOND_RUNS = ((0, 2), (2, 4), (4, 6), (6, 8), (8, 9))
 FIRST_BANKS = 6
-SECOND_BANKS = ((2, 3, 4, 5, 0), (5, 0, 5, 0, 5))
-VECTOR_BLOCKS = (13,)
-VECTOR_SECOND = ((0, 0), (0, 4), (0, 8))
+SECOND_BANKS = ((6, 7, 0, 1, 2), (3, 4, 5, 6, 7))
+VECTOR_BLOCKS = (13, 15)
+VECTOR_SECOND = ((0, 4), (0, 8))
 COMBINE_PIECES = ((0, 0, 384), (0, 384, 768), (1, 0, 384), (1, 384, 512), (1, 512, 768))
-SUM_BANKS = (5, 5, 4, 1)
-BACK_BANKS = (2, 3)
+SUM_BANKS = ((0, 1, 2), (4, 5, 6), (3, 1, 2), (7,))
+OWN_STORES = 2
+PACED = ()
+BACK_BANKS = (3, 7, 0, 4)
 
 
 def tile_moe_pkd_mlp_relu_kernel(
@@ -87,28 +93,38 @@ def tile_moe_pkd_mlp_relu_kernel(
                 in_=rows.unsqueeze(0).broadcast_to([8, 4, T // 4]),
             )
         nc.sync.dma_start(out=x_word_tile[:], in_=x_words[0].rearrange("p t r -> p (t r)").bitcast(I32))
-        w1_first = load_words(w1_words, 0, TURNED, "w1_first")
+        w1_first = load_words(w1_words, 0, FIRST, "w1_first")
         load_plane(w1_plane_early, w1_scales, 0, EARLY)
-        w1_early = load_words(w1_words, TURNED, EARLY, "w1_early")
+        w1_early = load_words(w1_words, FIRST, EARLY, "w1_early")
         load_plane(w1_plane_late, w1_scales, EARLY, E)
-        w1_late = load_words(w1_words, EARLY, E, "w1_late")
+        w1_middle = load_words(w1_words, EARLY, LATE, "w1_middle")
+        w1_late = load_words(w1_words, LATE, E, "w1_late")
         load_plane(w2_plane, w2_scales, 0, E)
         w2_tile = load_words(w2_words, 0, E, "w2_tile")
         for r, pos in enumerate((pos1, pos2, pos3)):
             nc.sync.dma_start(pos_sb[r][:], pos)
         nc.sync.dma_start(out=gate_sb[:], in_=gate[:, 0:P, :].rearrange("r p t -> p r t"))
 
-        def gather(window, dtype, runs, name):
+        def w1_as_loaded(first, end):
+            loads = ((w1_late, LATE), (w1_middle, EARLY), (w1_early, FIRST), (w1_first, 0))
+            words, base = [load for load in loads if load[1] <= first][0]
+            plane, plane_base = (w1_plane_late, EARLY) if first >= EARLY else (w1_plane_early, 0)
+            return (
+                words[:, (first - base) * 2 * H : (end - base) * 2 * H],
+                plane[:, (first - plane_base) * H : (end - plane_base) * H],
+            )
+
+        def gather(window, dtype, runs):
             blocks = []
             for count, buffer in runs:
                 start, width = len(blocks) * P, count * P
                 picks = offs_sb[:, start // LIST_ROWS : (start + width) // LIST_ROWS]
-                tile = sbuf.tile([P, width], dtype, name=f"{name}{buffer}", align_bytes=64)
+                tile = sbuf.tile([P, width], dtype, name=f"gathered{buffer}", align_bytes=64)
                 blocks.extend((tile, window, picks if c0 == 0 else None, c0) for c0 in range(0, width, P))
             return blocks
 
-        word_blocks = gather(x_word_tile[:].bitcast(U32), U32, WORD_GATHERS, "slot_words")
-        byte_blocks = gather(x_plane[:], U8, BYTE_GATHERS, "slot_scales")
+        word_blocks = gather(x_word_tile[:].bitcast(U32), U32, WORD_GATHERS)
+        byte_blocks = gather(x_plane[:], U8, BYTE_GATHERS)
 
         def slot_tokens(block):
             for tile, window, picks, c0 in (byte_blocks[block], word_blocks[block]):
@@ -119,12 +135,10 @@ def tile_moe_pkd_mlp_relu_kernel(
 
         w1_permuted = {}
         for first, end in PERMUTE_RUNS:
-            loaded, base = (w1_early, TURNED) if first < EARLY else (w1_late, EARLY)
-            raw_words = loaded[:, (first - base) * 2 * H : (end - base) * 2 * H]
-            plane, base = (w1_plane_early, 0) if first < EARLY else (w1_plane_late, EARLY)
-            raw_scales = plane[:, (first - base) * H : (end - base) * H]
+            raw_words, raw_scales = w1_as_loaded(first, end)
             words = sbuf.tile([P, (end - first) * 2 * H], U8, name=f"permuted_words{first}", align_bytes=64)
-            scales = sbuf.tile([P, (end - first) * H], U8, name=f"permuted_scales{first}", align_bytes=64)
+            name = "w1_middle" if first == LATE else f"permuted_scales{first}"
+            scales = sbuf.tile([P, (end - first) * H], U8, name=name, align_bytes=64)
             for dst, src in ((scales[:], raw_scales), (words[:].bitcast(U16), raw_words.bitcast(U16))):
                 nc.gpsimd.tensor_copy(
                     dst.rearrange("p (e t m) -> p e t m", t=PACK, m=P),
@@ -138,19 +152,20 @@ def tile_moe_pkd_mlp_relu_kernel(
         h_by_i = sbuf.tile([P, PACK * S], BF16, name="h_by_i", align_bytes=64)
 
         def first_layer(e):
-            if e < TURNED:
+            if e in TURNED:
                 h_by_slot[e] = sbuf.tile([P, 2, H], BF16, name=f"h_by_slot{e}", align_bytes=64)
             for b in range(2):
                 block = 2 * e + b
                 token_words, token_scales = slot_tokens(block)
                 acc = bank(block % FIRST_BANKS, H)
-                if e < TURNED:
+                if e in TURNED:
+                    words, scales = w1_as_loaded(e, e + 1)
                     nc.tensor.matmul_mx(
                         out=acc[:],
                         lhsT=token_words,
                         lhsT_scale=token_scales,
-                        rhs=w1_first[:, e * 2 * H : (e + 1) * 2 * H].bitcast(FP4X4),
-                        rhs_scale=w1_plane_early[:, e * H : (e + 1) * H],
+                        rhs=words.bitcast(FP4X4),
+                        rhs_scale=scales,
                         start=True,
                         stop=True,
                     )
@@ -184,14 +199,15 @@ def tile_moe_pkd_mlp_relu_kernel(
             for j in range(4):
                 nc.tensor.transpose(turned[:, j * P : (j + 1) * P], pairs[:, j * P : (j + 1) * P], ident[:])
             dst = h_by_i[:, e * PACK * C : (e + 1) * PACK * C].bitcast(F32).rearrange("p (b s u) -> p b s u", b=2, u=2)
-            nc.scalar.copy(dst, turned[:].rearrange("p (b u s) -> p b s u", b=2, u=2))
+            copy = nc.vector.tensor_copy if e in VECTOR_TURNS else nc.scalar.copy
+            copy(dst, turned[:].rearrange("p (b u s) -> p b s u", b=2, u=2))
 
         for e in range(E):
             first_layer(e)
-            if 1 <= e <= TURNED:
-                turn(e - 1)
+            if e - TURN_LAG in TURNED:
+                turn(e - TURN_LAG)
 
-        h_words = sbuf.tile([P, S], U32, name="x_word_tile", align_bytes=64)
+        h_words = sbuf.tile([P, S], U32, name="h_words", align_bytes=64)
         h_plane = sbuf.tile([P, S], U8, name="x_plane", align_bytes=64)
         for first, end in QUANTISE_RUNS:
             nc.vector.quantize_mx(
@@ -222,32 +238,35 @@ def tile_moe_pkd_mlp_relu_kernel(
             width = t1 - t0
             products = []
             for r in range(TOP):
-                product = sbuf.tile([P, width], F32, name=f"product{half}_{t0}_{r}")
+                name = f"by_token{piece - 2}" if r == 0 and piece in PACED else f"product{piece}_{r}"
+                product = sbuf.tile([P, width], F32, name=name)
                 picks = pos_sb[r][:, t0 // LIST_ROWS : t1 // LIST_ROWS]
                 nc.vector.tensor_tensor(product[:], y[half][:].indirect(picks), gate_sb[:, r, t0:t1], MULT)
                 products.append(product)
             out_piece = out[half * P : (half + 1) * P, t0:t1]
             if (half, t0, t1) == COMBINE_PIECES[-1]:
                 nc.vector.tensor_tensor(products[0][:], products[0][:], products[1][:], ADD)
-                nc.vector.tensor_tensor(products[2][:], products[0][:], products[2][:], ADD)
-                nc.sync.dma_start(out=out_piece, in_=products[2][:])
+                total = sbuf.tile([P, width], F32, name="total")
+                nc.vector.tensor_tensor(total[:], products[0][:], products[2][:], ADD)
+                nc.sync.dma_start(out=out_piece, in_=total[:])
                 continue
-            summed = bank(SUM_BANKS[piece], width)
-            for c0 in range(0, width, P):
-                for r in range(TOP):
+            sums = [bank(number, P) for number in SUM_BANKS[piece]]
+            for r in range(TOP):
+                for j, summed in enumerate(sums):
                     nc.tensor.matmul(
-                        summed[:, c0 : c0 + P],
-                        lhsT=products[r][:, c0 : c0 + P],
+                        summed[:],
+                        lhsT=products[r][:, j * P : (j + 1) * P],
                         rhs=ident[:],
                         is_transpose=True,
                         start=(r == 0),
                         stop=(r == TOP - 1),
                     )
-            by_token = sbuf.tile([P, width], F32, name=f"by_token{half}_{t0}")
-            nc.scalar.copy(by_token[:], summed[:])
-            back = bank(BACK_BANKS[piece % 2], width)
+            by_token = sbuf.tile([P, width], F32, name=f"by_token{piece}")
+            for j, summed in enumerate(sums):
+                nc.scalar.copy(by_token[:, j * P : (j + 1) * P], summed[:])
+            back = bank(BACK_BANKS[piece], width)
             for c0 in range(0, width, P):
                 nc.tensor.transpose(back[:, c0 : c0 + P], by_token[:, c0 : c0 + P], ident[:])
             result = sbuf.tile([P, width], F32, name=f"result{half}_{t0}")
             nc.scalar.copy(result[:], back[:])
-            nc.scalar.dma_start(out=out_piece, in_=result[:])
+            (nc.scalar if piece >= OWN_STORES else nc.sync).dma_start(out=out_piece, in_=result[:])

@@ -23,8 +23,8 @@ RELU = mybir.ActivationFunctionType.Relu
 MULT = mybir.AluOpType.mult
 ADD = mybir.AluOpType.add
 
-WORD_GATHERS = ((1, 0), (1, 1), (2, 2), (2, 3), (4, 1), (4, 2), (4, 3))
-BYTE_GATHERS = ((2, 4), (2, 5), (2, 0), (4, 4), (4, 5), (4, 0))
+WORD_GATHERS = ((1, 0), (2, 1), (3, 2), (6, 1), (6, 2))
+BYTE_GATHERS = ((6, 3), (6, 0), (6, 3))
 TURNED = (0, 1, 2)
 FIRST = 2
 LATE = 6
@@ -34,15 +34,19 @@ EARLY = 4
 PERMUTE_RUNS = ((3, 4), (4, 6), (6, 8), (8, 9))
 QUANTISE_RUNS = ((0, 2), (2, 4), (4, 6), (6, 8), (8, 9))
 SECOND_RUNS = ((0, 2), (2, 4), (4, 6), (6, 8), (8, 9))
-FIRST_BANKS = 6
-SECOND_BANKS = ((6, 7, 0, 1, 2), (3, 4, 5, 6, 7))
-VECTOR_BLOCKS = (13, 15)
+FIRST_BANKS = 8
+SECOND_BANKS = ((2, 3, 4, 5, 6), (7, 6, 7, 6, 7))
+VECTOR_BLOCKS = (11, 13)
 VECTOR_SECOND = ((0, 4), (0, 8))
-COMBINE_PIECES = ((0, 0, 384), (0, 384, 768), (1, 0, 384), (1, 384, 512), (1, 512, 768))
-SUM_BANKS = ((0, 1, 2), (4, 5, 6), (3, 1, 2), (7,))
-OWN_STORES = 2
+COMBINE_PIECES = ((0, 0, 768), (1, 0, 512), (1, 512, 768))
+SUM_BANKS = ((0, 1, 2, 3, 4, 5), (0, 1, 2, 3))
+OWN_STORES = 1
+H_WORDS = "w1_late"
+WINDOW = 1024
+TURN_BANKS = (6, 7, 0)
+LAST_PART = 128
 PACED = ()
-BACK_BANKS = (3, 7, 0, 4)
+BACK_BANKS = (((0, 384, 6), (384, 768, 7)), ((0, 256, 4), (256, 512, 5)))
 
 
 def tile_moe_pkd_mlp_relu_kernel(
@@ -58,8 +62,8 @@ def tile_moe_pkd_mlp_relu_kernel(
 
         offs_sb = sbuf.tile([P, S // LIST_ROWS], U16, name="offs_sb")
         pos_sb = [sbuf.tile([P, T // LIST_ROWS], U16, name=f"pos_sb{r}") for r in range(TOP)]
-        x_word_tile = sbuf.tile([P, T], I32, name="x_word_tile", align_bytes=64)
-        x_plane = sbuf.tile([P, T], U8, name="x_plane", align_bytes=64)
+        x_word_tile = sbuf.tile([P, WINDOW], I32, name="x_word_tile", align_bytes=64)
+        x_plane = sbuf.tile([P, WINDOW], U8, name="x_plane", align_bytes=64)
         w1_plane_early = sbuf.tile([P, EARLY * H], U8, name="w1_plane_early", align_bytes=64)
         w1_plane_late = sbuf.tile([P, (E - EARLY) * H], U8, name="w1_plane_late", align_bytes=64)
         w2_plane = sbuf.tile([P, E * N], U8, name="w2_plane", align_bytes=64)
@@ -68,46 +72,46 @@ def tile_moe_pkd_mlp_relu_kernel(
 
         for plane in (w1_plane_early, w1_plane_late, w2_plane):
             nc.gpsimd.memset(plane[:].bitcast(I32), 0)
+        nc.vector.memset(x_word_tile[:, T:WINDOW], 0)
+        nc.vector.memset(x_plane[:].bitcast(I32)[:, T // 4 : WINDOW // 4], 0)
         make_identity(nc, ident[:])
 
         def load_plane(plane, scales, first, end):
-            for q in range(4):
+            for r in range(4):
                 nc.sync.dma_start(
-                    out=plane[32 * q : 32 * q + 4, :].bitcast(I32).rearrange("r (e w) -> r e w", e=end - first),
-                    in_=scales[first:end, 0, 4 * q : 4 * q + 4, :].rearrange("e r w -> r e w").bitcast(I32),
+                    out=plane[r:P:32, :].bitcast(I32).rearrange("q (e w) -> q e w", e=end - first),
+                    in_=scales[first:end, 0, r:16:4, :].rearrange("e q w -> q e w").bitcast(I32),
                 )
 
-        def load_words(words, first, end, name):
-            tile = sbuf.tile([P, (end - first) * words.shape[-1]], U8, name=name, align_bytes=64)
-            nc.sync.dma_start(
-                out=tile[:].bitcast(I32).rearrange("p (e w) -> p e w", e=end - first),
-                in_=words[first:end, 0].rearrange("e p w -> p e w").bitcast(I32),
-            )
+        def load_words(words, experts, name):
+            source = words[experts, 0].rearrange("e p w -> p e w").bitcast(I32)
+            tile = sbuf.tile([P, source.shape[1] * words.shape[-1]], U8, name=name, align_bytes=64)
+            nc.sync.dma_start(out=tile[:].bitcast(I32).rearrange("p (e w) -> p e w", e=source.shape[1]), in_=source)
             return tile
 
         nc.sync.dma_start(offs_sb[:], offs)
         for q in range(4):
             rows = x_scales[0, 4 * q : 4 * q + 4, :].bitcast(I32)
             (nc.sync if q < 2 else nc.scalar).dma_start(
-                out=x_plane[32 * q : 32 * q + 32, :].bitcast(I32),
+                out=x_plane[32 * q : 32 * q + 32, 0:T].bitcast(I32),
                 in_=rows.unsqueeze(0).broadcast_to([8, 4, T // 4]),
             )
-        nc.sync.dma_start(out=x_word_tile[:], in_=x_words[0].rearrange("p t r -> p (t r)").bitcast(I32))
-        w1_first = load_words(w1_words, 0, FIRST, "w1_first")
+        nc.sync.dma_start(out=x_word_tile[:, 0:T], in_=x_words[0].rearrange("p t r -> p (t r)").bitcast(I32))
+        w1_first = load_words(w1_words, slice(0, 4, 3), "w1_first")
         load_plane(w1_plane_early, w1_scales, 0, EARLY)
-        w1_early = load_words(w1_words, FIRST, EARLY, "w1_early")
+        w1_turned = load_words(w1_words, slice(1, 3), "w1_turned")
+        w1_early = load_words(w1_words, slice(4, LATE), "w1_early")
         load_plane(w1_plane_late, w1_scales, EARLY, E)
-        w1_middle = load_words(w1_words, EARLY, LATE, "w1_middle")
-        w1_late = load_words(w1_words, LATE, E, "w1_late")
+        w1_late = load_words(w1_words, slice(LATE, E), "w1_late")
         load_plane(w2_plane, w2_scales, 0, E)
-        w2_tile = load_words(w2_words, 0, E, "w2_tile")
+        w2_tile = load_words(w2_words, slice(0, E), "w2_tile")
         for r, pos in enumerate((pos1, pos2, pos3)):
             nc.sync.dma_start(pos_sb[r][:], pos)
         nc.sync.dma_start(out=gate_sb[:], in_=gate[:, 0:P, :].rearrange("r p t -> p r t"))
 
         def w1_as_loaded(first, end):
-            loads = ((w1_late, LATE), (w1_middle, EARLY), (w1_early, FIRST), (w1_first, 0))
-            words, base = [load for load in loads if load[1] <= first][0]
+            loads = ((w1_late, LATE, LATE), (w1_early, 4, 4), (w1_first, 3, 2), (w1_turned, 1, 1), (w1_first, 0, 0))
+            words, least, base = [load for load in loads if load[1] <= first][0]
             plane, plane_base = (w1_plane_late, EARLY) if first >= EARLY else (w1_plane_early, 0)
             return (
                 words[:, (first - base) * 2 * H : (end - base) * 2 * H],
@@ -137,8 +141,7 @@ def tile_moe_pkd_mlp_relu_kernel(
         for first, end in PERMUTE_RUNS:
             raw_words, raw_scales = w1_as_loaded(first, end)
             words = sbuf.tile([P, (end - first) * 2 * H], U8, name=f"permuted_words{first}", align_bytes=64)
-            name = "w1_middle" if first == LATE else f"permuted_scales{first}"
-            scales = sbuf.tile([P, (end - first) * H], U8, name=name, align_bytes=64)
+            scales = sbuf.tile([P, (end - first) * H], U8, name=f"permuted_scales{first}", align_bytes=64)
             for dst, src in ((scales[:], raw_scales), (words[:].bitcast(U16), raw_words.bitcast(U16))):
                 nc.gpsimd.tensor_copy(
                     dst.rearrange("p (e t m) -> p e t m", t=PACK, m=P),
@@ -195,7 +198,7 @@ def tile_moe_pkd_mlp_relu_kernel(
 
         def turn(e):
             pairs = h_by_slot[e][:].rearrange("s b i -> s (b i)").bitcast(F32)
-            turned = bank(FIRST_BANKS + e % 2, 4 * P)
+            turned = bank(TURN_BANKS[e], 4 * P)
             for j in range(4):
                 nc.tensor.transpose(turned[:, j * P : (j + 1) * P], pairs[:, j * P : (j + 1) * P], ident[:])
             dst = h_by_i[:, e * PACK * C : (e + 1) * PACK * C].bitcast(F32).rearrange("p (b s u) -> p b s u", b=2, u=2)
@@ -204,10 +207,11 @@ def tile_moe_pkd_mlp_relu_kernel(
 
         for e in range(E):
             first_layer(e)
-            if e - TURN_LAG in TURNED:
-                turn(e - TURN_LAG)
+            for done in TURNED:
+                if e == len(TURNED) - 1:
+                    turn(done)
 
-        h_words = sbuf.tile([P, S], U32, name="h_words", align_bytes=64)
+        h_words = sbuf.tile([P, S], U32, name=H_WORDS, align_bytes=64)
         h_plane = sbuf.tile([P, S], U8, name="x_plane", align_bytes=64)
         for first, end in QUANTISE_RUNS:
             nc.vector.quantize_mx(
@@ -245,10 +249,12 @@ def tile_moe_pkd_mlp_relu_kernel(
                 products.append(product)
             out_piece = out[half * P : (half + 1) * P, t0:t1]
             if (half, t0, t1) == COMBINE_PIECES[-1]:
-                nc.vector.tensor_tensor(products[0][:], products[0][:], products[1][:], ADD)
-                total = sbuf.tile([P, width], F32, name="total")
-                nc.vector.tensor_tensor(total[:], products[0][:], products[2][:], ADD)
-                nc.sync.dma_start(out=out_piece, in_=total[:])
+                parts = [slice(c0, c0 + LAST_PART) for c0 in range(0, width, LAST_PART)]
+                for part in parts:
+                    nc.vector.tensor_tensor(products[0][:, part], products[0][:, part], products[1][:, part], ADD)
+                for part in parts:
+                    nc.vector.tensor_tensor(products[2][:, part], products[0][:, part], products[2][:, part], ADD)
+                    nc.sync.dma_start(out=out_piece[:, part], in_=products[2][:, part])
                 continue
             sums = [bank(number, P) for number in SUM_BANKS[piece]]
             for r in range(TOP):
@@ -264,9 +270,10 @@ def tile_moe_pkd_mlp_relu_kernel(
             by_token = sbuf.tile([P, width], F32, name=f"by_token{piece}")
             for j, summed in enumerate(sums):
                 nc.scalar.copy(by_token[:, j * P : (j + 1) * P], summed[:])
-            back = bank(BACK_BANKS[piece], width)
-            for c0 in range(0, width, P):
-                nc.tensor.transpose(back[:, c0 : c0 + P], by_token[:, c0 : c0 + P], ident[:])
-            result = sbuf.tile([P, width], F32, name=f"result{half}_{t0}")
-            nc.scalar.copy(result[:], back[:])
-            (nc.scalar if piece >= OWN_STORES else nc.sync).dma_start(out=out_piece, in_=result[:])
+            for c0, c1, number in BACK_BANKS[piece]:
+                back = bank(number, c1 - c0)
+                for c in range(c0, c1, P):
+                    nc.tensor.transpose(back[:, c - c0 : c - c0 + P], by_token[:, c : c + P], ident[:])
+                result = sbuf.tile([P, c1 - c0], F32, name=f"result{piece}_{c0}")
+                nc.scalar.copy(result[:], back[:])
+                (nc.scalar if piece >= OWN_STORES else nc.sync).dma_start(out=out_piece[:, c0:c1], in_=result[:])

@@ -24,29 +24,30 @@ MULT = mybir.AluOpType.mult
 ADD = mybir.AluOpType.add
 
 WORD_GATHERS = ((1, 0), (2, 1), (3, 2), (6, 1), (6, 2))
-BYTE_GATHERS = ((6, 3), (6, 0), (6, 3))
-TURNED = (0, 1, 2)
-FIRST = 2
+BYTE_GATHERS = ((4, 3), (4, 0), (6, 3), (4, 0))
+TURNED = (0, 1)
+NT = len(TURNED)
 LATE = 6
 TURN_LAG = 2
 VECTOR_TURNS = ()
-EARLY = 4
-PERMUTE_RUNS = ((3, 4), (4, 6), (6, 8), (8, 9))
+EARLY = 3
+PERMUTE_RUNS = ((2, 3), (3, 6), (6, 8), (8, 9))
 QUANTISE_RUNS = ((0, 2), (2, 4), (4, 6), (6, 8), (8, 9))
 SECOND_RUNS = ((0, 2), (2, 4), (4, 6), (6, 8), (8, 9))
+FIRST_PAIRS = (0, 1, 1, 2, 0, 3, 1, 2, 0)
 FIRST_BANKS = 8
-SECOND_BANKS = ((2, 3, 4, 5, 6), (7, 6, 7, 6, 7))
+SECOND_BANKS = ((6, 7, 2, 3, 4), (5, 4, 5, 4, 5))
 VECTOR_BLOCKS = (11, 13)
 VECTOR_SECOND = ((0, 4), (0, 8))
 COMBINE_PIECES = ((0, 0, 768), (1, 0, 512), (1, 512, 768))
-SUM_BANKS = ((0, 1, 2, 3, 4, 5), (0, 1, 2, 3))
+SUM_BANKS = ((0, 1, 2, 3, 6, 7), (0, 1, 2, 3))
 OWN_STORES = 1
 H_WORDS = "w1_late"
 WINDOW = 1024
-TURN_BANKS = (6, 7, 0)
+TURN_BANKS = (6, 7)
 LAST_PART = 128
 PACED = ()
-BACK_BANKS = (((0, 384, 6), (384, 768, 7)), ((0, 256, 4), (256, 512, 5)))
+BACK_BANKS = (((0, 384, 4), (384, 768, 5)), ((0, 256, 6), (256, 512, 7)))
 
 
 def tile_moe_pkd_mlp_relu_kernel(
@@ -97,10 +98,9 @@ def tile_moe_pkd_mlp_relu_kernel(
                 in_=rows.unsqueeze(0).broadcast_to([8, 4, T // 4]),
             )
         nc.sync.dma_start(out=x_word_tile[:, 0:T], in_=x_words[0].rearrange("p t r -> p (t r)").bitcast(I32))
-        w1_first = load_words(w1_words, slice(0, 4, 3), "w1_first")
+        w1_first = load_words(w1_words, slice(0, EARLY), "w1_first")
         load_plane(w1_plane_early, w1_scales, 0, EARLY)
-        w1_turned = load_words(w1_words, slice(1, 3), "w1_turned")
-        w1_early = load_words(w1_words, slice(4, LATE), "w1_early")
+        w1_early = load_words(w1_words, slice(EARLY, LATE), "w1_early")
         load_plane(w1_plane_late, w1_scales, EARLY, E)
         w1_late = load_words(w1_words, slice(LATE, E), "w1_late")
         load_plane(w2_plane, w2_scales, 0, E)
@@ -110,7 +110,7 @@ def tile_moe_pkd_mlp_relu_kernel(
         nc.sync.dma_start(out=gate_sb[:], in_=gate[:, 0:P, :].rearrange("r p t -> p r t"))
 
         def w1_as_loaded(first, end):
-            loads = ((w1_late, LATE, LATE), (w1_early, 4, 4), (w1_first, 3, 2), (w1_turned, 1, 1), (w1_first, 0, 0))
+            loads = ((w1_late, LATE, LATE), (w1_early, EARLY, EARLY), (w1_first, 0, 0))
             words, least, base = [load for load in loads if load[1] <= first][0]
             plane, plane_base = (w1_plane_late, EARLY) if first >= EARLY else (w1_plane_early, 0)
             return (
@@ -160,7 +160,7 @@ def tile_moe_pkd_mlp_relu_kernel(
             for b in range(2):
                 block = 2 * e + b
                 token_words, token_scales = slot_tokens(block)
-                acc = bank(block % FIRST_BANKS, H)
+                acc = bank(2 * FIRST_PAIRS[e] + b, H)
                 if e in TURNED:
                     words, scales = w1_as_loaded(e, e + 1)
                     nc.tensor.matmul_mx(

@@ -37,17 +37,21 @@ SECOND_RUNS = ((0, 2), (2, 4), (4, 6), (6, 8), (8, 9))
 FIRST_PAIRS = (0, 1, 1, 2, 0, 3, 1, 2, 0)
 FIRST_BANKS = 8
 SECOND_BANKS = ((6, 7, 2, 3, 4), (5, 4, 5, 4, 5))
-VECTOR_BLOCKS = (11, 13)
+VECTOR_BLOCKS = (12, 13)
 VECTOR_SECOND = ((0, 4), (0, 8))
-COMBINE_PIECES = ((0, 0, 768), (1, 0, 512), (1, 512, 768))
-SUM_BANKS = ((0, 1, 2, 3, 6, 7), (0, 1, 2, 3))
+COMBINE_PIECES = ((0, 0, 768), (1, 0, 384), (1, 384, 768))
+SUM_BANKS = ((0, 1, 2, 3, 6, 7), (0, 1, 2))
 OWN_STORES = 1
 H_WORDS = "w1_late"
 WINDOW = 1024
 TURN_BANKS = (6, 7)
-LAST_PART = 128
+LAST_PART = 192
+BYTE_WINDOW = 1024
+CUT = 0
+CUT_PIECE = 0
+SWAPPED = (1, 4, 5, 8)
 PACED = ()
-BACK_BANKS = (((0, 384, 4), (384, 768, 5)), ((0, 256, 6), (256, 512, 7)))
+BACK_BANKS = (((0, 384, 4), (384, 768, 5)), ((0, 384, 6),))
 
 
 def tile_moe_pkd_mlp_relu_kernel(
@@ -64,7 +68,7 @@ def tile_moe_pkd_mlp_relu_kernel(
         offs_sb = sbuf.tile([P, S // LIST_ROWS], U16, name="offs_sb")
         pos_sb = [sbuf.tile([P, T // LIST_ROWS], U16, name=f"pos_sb{r}") for r in range(TOP)]
         x_word_tile = sbuf.tile([P, WINDOW], I32, name="x_word_tile", align_bytes=64)
-        x_plane = sbuf.tile([P, WINDOW], U8, name="x_plane", align_bytes=64)
+        x_plane = sbuf.tile([P, BYTE_WINDOW], U8, name="x_plane", align_bytes=64)
         w1_plane_early = sbuf.tile([P, EARLY * H], U8, name="w1_plane_early", align_bytes=64)
         w1_plane_late = sbuf.tile([P, (E - EARLY) * H], U8, name="w1_plane_late", align_bytes=64)
         w2_plane = sbuf.tile([P, E * N], U8, name="w2_plane", align_bytes=64)
@@ -74,7 +78,7 @@ def tile_moe_pkd_mlp_relu_kernel(
         for plane in (w1_plane_early, w1_plane_late, w2_plane):
             nc.gpsimd.memset(plane[:].bitcast(I32), 0)
         nc.vector.memset(x_word_tile[:, T:WINDOW], 0)
-        nc.vector.memset(x_plane[:].bitcast(I32)[:, T // 4 : WINDOW // 4], 0)
+        nc.vector.memset(x_plane[:].bitcast(I32)[:, T // 4 : BYTE_WINDOW // 4], 0)
         make_identity(nc, ident[:])
 
         def load_plane(plane, scales, first, end):
@@ -157,6 +161,7 @@ def tile_moe_pkd_mlp_relu_kernel(
         def first_layer(e):
             if e in TURNED:
                 h_by_slot[e] = sbuf.tile([P, 2, H], BF16, name=f"h_by_slot{e}", align_bytes=64)
+            empties = []
             for b in range(2):
                 block = 2 * e + b
                 token_words, token_scales = slot_tokens(block)
@@ -172,11 +177,8 @@ def tile_moe_pkd_mlp_relu_kernel(
                         start=True,
                         stop=True,
                     )
-                    nc.scalar.activation(
-                        h_by_slot[e][:, b, :].rearrange("s (u p d) -> s u p d", u=2, d=2),
-                        acc[:].rearrange("s (p u d) -> s u p d", u=2, d=2),
-                        RELU,
-                    )
+                    dst = h_by_slot[e][:, b, :].rearrange("s (u p d) -> s u p d", u=2, d=2)
+                    src = acc[:].rearrange("s (p u d) -> s u p d", u=2, d=2)
                 else:
                     words, scales = w1_permuted[e]
                     for t in range(PACK):
@@ -191,10 +193,12 @@ def tile_moe_pkd_mlp_relu_kernel(
                         )
                     dst = h_by_i[:, block * H : (block + 1) * H].rearrange("p (s t) -> p s t", t=PACK)
                     src = acc[:].rearrange("p (t s) -> p s t", t=PACK)
-                    if block in VECTOR_BLOCKS:
-                        nc.vector.tensor_scalar_max(dst, src, 0.0)
-                    else:
-                        nc.scalar.activation(dst, src, RELU)
+                empties.append((block, dst, src))
+            for block, dst, src in (empties[::-1] if e in SWAPPED else empties):
+                if block in VECTOR_BLOCKS:
+                    nc.vector.tensor_scalar_max(dst, src, 0.0)
+                else:
+                    nc.scalar.activation(dst, src, RELU)
 
         def turn(e):
             pairs = h_by_slot[e][:].rearrange("s b i -> s (b i)").bitcast(F32)
@@ -244,8 +248,10 @@ def tile_moe_pkd_mlp_relu_kernel(
             for r in range(TOP):
                 name = f"by_token{piece - 2}" if r == 0 and piece in PACED else f"product{piece}_{r}"
                 product = sbuf.tile([P, width], F32, name=name)
-                picks = pos_sb[r][:, t0 // LIST_ROWS : t1 // LIST_ROWS]
-                nc.vector.tensor_tensor(product[:], y[half][:].indirect(picks), gate_sb[:, r, t0:t1], MULT)
+                cuts = (t0, t0 + CUT, t1) if CUT and piece == CUT_PIECE and r == TOP - 1 else (t0, t1)
+                for c0, c1 in zip(cuts, cuts[1:]):
+                    picks = pos_sb[r][:, c0 // LIST_ROWS : c1 // LIST_ROWS]
+                    nc.vector.tensor_tensor(product[:, c0 - t0 : c1 - t0], y[half][:].indirect(picks), gate_sb[:, r, c0:c1], MULT)
                 products.append(product)
             out_piece = out[half * P : (half + 1) * P, t0:t1]
             if (half, t0, t1) == COMBINE_PIECES[-1]:

@@ -23,35 +23,22 @@ RELU = mybir.ActivationFunctionType.Relu
 MULT = mybir.AluOpType.mult
 ADD = mybir.AluOpType.add
 
-WORD_GATHERS = ((1, 0), (2, 1), (3, 2), (6, 1), (6, 2))
-BYTE_GATHERS = ((4, 3), (4, 0), (6, 3), (4, 0))
-TURNED = (0, 1)
-NT = len(TURNED)
-LATE = 6
-TURN_LAG = 2
-VECTOR_TURNS = ()
-EARLY = 3
-PERMUTE_RUNS = ((2, 3), (3, 6), (6, 8), (8, 9))
-QUANTISE_RUNS = ((0, 2), (2, 4), (4, 6), (6, 8), (8, 9))
-SECOND_RUNS = ((0, 2), (2, 4), (4, 6), (6, 8), (8, 9))
-FIRST_PAIRS = (0, 1, 1, 2, 0, 3, 1, 2, 0)
-FIRST_BANKS = 8
-SECOND_BANKS = ((6, 7, 2, 3, 4), (5, 4, 5, 4, 5))
-VECTOR_BLOCKS = (12, 13)
-VECTOR_SECOND = ((0, 4), (0, 8))
-COMBINE_PIECES = ((0, 0, 768), (1, 0, 384), (1, 384, 768))
-SUM_BANKS = ((0, 1, 2, 3, 6, 7), (0, 1, 2))
-OWN_STORES = 1
-H_WORDS = "w1_late"
+COPY = mybir.ActivationFunctionType.Copy
+
+BLOCKS = S // P
+BANKS = 8
 WINDOW = 1024
-TURN_BANKS = (6, 7)
+WIDEST = 3 * WINDOW // (4 * P)
+FIRST_BYTES = 4
+GATHER_BUFFERS = 4
+TURNED = 2
+EARLY, LATE = 3, 6
+PERMUTE_RUNS = ((TURNED, EARLY), (EARLY, LATE), (LATE, E - 1), (E - 1, E))
+PAIRS = tuple((e, min(e + 2, E)) for e in range(0, E, 2))
+VECTOR_EXPERT = 6
+VECTOR_RUNS = (2, 4)
+SPLIT = 384
 LAST_PART = 192
-BYTE_WINDOW = 1024
-CUT = 0
-CUT_PIECE = 0
-SWAPPED = (1, 4, 5, 8)
-PACED = ()
-BACK_BANKS = (((0, 384, 4), (384, 768, 5)), ((0, 384, 6),))
 
 
 def tile_moe_pkd_mlp_relu_kernel(
@@ -62,13 +49,18 @@ def tile_moe_pkd_mlp_relu_kernel(
         sbuf = ctx.enter_context(tc.tile_pool(name="sbuf", bufs=1))
         psum = ctx.enter_context(tc.psum_pool(name="psum", bufs=1))
 
-        def bank(number, width):
-            return psum.tile([P, width], F32, name=f"bank{number}")
+        by_age = list(range(BANKS))
+
+        def bank(width, number=None):
+            number = by_age[0] if number is None else number
+            by_age.remove(number)
+            by_age.append(number)
+            return psum.tile([P, width], F32, name=f"bank{number}"), number
 
         offs_sb = sbuf.tile([P, S // LIST_ROWS], U16, name="offs_sb")
         pos_sb = [sbuf.tile([P, T // LIST_ROWS], U16, name=f"pos_sb{r}") for r in range(TOP)]
         x_word_tile = sbuf.tile([P, WINDOW], I32, name="x_word_tile", align_bytes=64)
-        x_plane = sbuf.tile([P, BYTE_WINDOW], U8, name="x_plane", align_bytes=64)
+        x_plane = sbuf.tile([P, WINDOW], U8, name="x_plane", align_bytes=64)
         w1_plane_early = sbuf.tile([P, EARLY * H], U8, name="w1_plane_early", align_bytes=64)
         w1_plane_late = sbuf.tile([P, (E - EARLY) * H], U8, name="w1_plane_late", align_bytes=64)
         w2_plane = sbuf.tile([P, E * N], U8, name="w2_plane", align_bytes=64)
@@ -78,7 +70,7 @@ def tile_moe_pkd_mlp_relu_kernel(
         for plane in (w1_plane_early, w1_plane_late, w2_plane):
             nc.gpsimd.memset(plane[:].bitcast(I32), 0)
         nc.vector.memset(x_word_tile[:, T:WINDOW], 0)
-        nc.vector.memset(x_plane[:].bitcast(I32)[:, T // 4 : BYTE_WINDOW // 4], 0)
+        nc.vector.memset(x_plane[:].bitcast(I32)[:, T // 4 : WINDOW // 4], 0)
         make_identity(nc, ident[:])
 
         def load_plane(plane, scales, first, end):
@@ -122,24 +114,26 @@ def tile_moe_pkd_mlp_relu_kernel(
                 plane[:, (first - plane_base) * H : (end - plane_base) * H],
             )
 
-        def gather(window, dtype, runs):
-            blocks = []
-            for count, buffer in runs:
-                start, width = len(blocks) * P, count * P
-                picks = offs_sb[:, start // LIST_ROWS : (start + width) // LIST_ROWS]
-                tile = sbuf.tile([P, width], dtype, name=f"gathered{buffer}", align_bytes=64)
-                blocks.extend((tile, window, picks if c0 == 0 else None, c0) for c0 in range(0, width, P))
-            return blocks
+        last_reader = [-1] * GATHER_BUFFERS
+        slot_words, slot_bytes = [], []
 
-        word_blocks = gather(x_word_tile[:].bitcast(U32), U32, WORD_GATHERS)
-        byte_blocks = gather(x_plane[:], U8, BYTE_GATHERS)
+        def gather(window, dtype, blocks, count):
+            start = len(blocks)
+            buffer = last_reader.index(min(last_reader))
+            last_reader[buffer] = start + count - 1
+            tile = sbuf.tile([P, count * P], dtype, name=f"gathered{buffer}", align_bytes=64)
+            picks = offs_sb[:, start * P // LIST_ROWS : (start + count) * P // LIST_ROWS]
+            nc.vector.tensor_copy(tile[:], window.indirect(picks))
+            blocks.extend(tile[:, c * P : (c + 1) * P] for c in range(count))
 
         def slot_tokens(block):
-            for tile, window, picks, c0 in (byte_blocks[block], word_blocks[block]):
-                if picks is not None:
-                    nc.vector.tensor_copy(tile[:], window.indirect(picks))
-            words, scales = word_blocks[block], byte_blocks[block]
-            return words[0][:, words[3] : words[3] + P].bitcast(FP8X4), scales[0][:, scales[3] : scales[3] + P]
+            if block == len(slot_bytes):
+                reach = FIRST_BYTES if block == 0 else min(len(slot_words) + 2, BLOCKS)
+                gather(x_plane[:], U8, slot_bytes, reach - block)
+            if block == len(slot_words):
+                count = WIDEST if block >= WIDEST else 1 + (block + 1) // 2
+                gather(x_word_tile[:].bitcast(U32), U32, slot_words, count)
+            return slot_words[block].bitcast(FP8X4), slot_bytes[block]
 
         w1_permuted = {}
         for first, end in PERMUTE_RUNS:
@@ -158,15 +152,16 @@ def tile_moe_pkd_mlp_relu_kernel(
         h_by_slot = {}
         h_by_i = sbuf.tile([P, PACK * S], BF16, name="h_by_i", align_bytes=64)
 
+        first_banks = {}
+
         def first_layer(e):
-            if e in TURNED:
+            if e < TURNED:
                 h_by_slot[e] = sbuf.tile([P, 2, H], BF16, name=f"h_by_slot{e}", align_bytes=64)
-            empties = []
             for b in range(2):
                 block = 2 * e + b
                 token_words, token_scales = slot_tokens(block)
-                acc = bank(2 * FIRST_PAIRS[e] + b, H)
-                if e in TURNED:
+                acc, first_banks[block] = bank(H, first_banks[block - 2] if e == TURNED else None)
+                if e < TURNED:
                     words, scales = w1_as_loaded(e, e + 1)
                     nc.tensor.matmul_mx(
                         out=acc[:],
@@ -193,31 +188,28 @@ def tile_moe_pkd_mlp_relu_kernel(
                         )
                     dst = h_by_i[:, block * H : (block + 1) * H].rearrange("p (s t) -> p s t", t=PACK)
                     src = acc[:].rearrange("p (t s) -> p s t", t=PACK)
-                empties.append((block, dst, src))
-            for block, dst, src in (empties[::-1] if e in SWAPPED else empties):
-                if block in VECTOR_BLOCKS:
+                if e == VECTOR_EXPERT:
                     nc.vector.tensor_scalar_max(dst, src, 0.0)
                 else:
                     nc.scalar.activation(dst, src, RELU)
 
         def turn(e):
             pairs = h_by_slot[e][:].rearrange("s b i -> s (b i)").bitcast(F32)
-            turned = bank(TURN_BANKS[e], 4 * P)
+            turned = bank(4 * P)[0]
             for j in range(4):
                 nc.tensor.transpose(turned[:, j * P : (j + 1) * P], pairs[:, j * P : (j + 1) * P], ident[:])
             dst = h_by_i[:, e * PACK * C : (e + 1) * PACK * C].bitcast(F32).rearrange("p (b s u) -> p b s u", b=2, u=2)
-            copy = nc.vector.tensor_copy if e in VECTOR_TURNS else nc.scalar.copy
-            copy(dst, turned[:].rearrange("p (b u s) -> p b s u", b=2, u=2))
+            nc.scalar.copy(dst, turned[:].rearrange("p (b u s) -> p b s u", b=2, u=2))
 
         for e in range(E):
             first_layer(e)
-            for done in TURNED:
-                if e == len(TURNED) - 1:
+            if e == TURNED - 1:
+                for done in range(TURNED):
                     turn(done)
 
-        h_words = sbuf.tile([P, S], U32, name=H_WORDS, align_bytes=64)
+        h_words = sbuf.tile([P, S], U32, name="w1_late", align_bytes=64)
         h_plane = sbuf.tile([P, S], U8, name="x_plane", align_bytes=64)
-        for first, end in QUANTISE_RUNS:
+        for first, end in PAIRS:
             nc.vector.quantize_mx(
                 out=h_words[:, first * C : end * C].bitcast(FP8X4),
                 scales=h_plane[:, first * C : end * C],
@@ -225,9 +217,11 @@ def tile_moe_pkd_mlp_relu_kernel(
             )
 
         y = [sbuf.tile([P, S], F32, name=f"y{half}") for half in range(2)]
+        second_banks = []
         for half in range(2):
-            for (first, end), number in zip(SECOND_RUNS, SECOND_BANKS[half]):
-                acc = bank(number, (end - first) * C)
+            for run, (first, end) in enumerate(PAIRS):
+                acc, number = bank((end - first) * C, second_banks[-2] if half and run else None)
+                second_banks.append(number)
                 for e in range(first, end):
                     col = e * N + half * P
                     nc.tensor.matmul_mx(
@@ -239,47 +233,62 @@ def tile_moe_pkd_mlp_relu_kernel(
                         start=True,
                         stop=True,
                     )
-                copy = nc.vector.tensor_copy if (half, first) in VECTOR_SECOND else nc.scalar.copy
+                copy = nc.vector.tensor_copy if half == 0 and run in VECTOR_RUNS else nc.scalar.copy
                 copy(y[half][:, first * C : end * C], acc[:])
 
-        for piece, (half, t0, t1) in enumerate(COMBINE_PIECES):
-            width = t1 - t0
-            products = []
-            for r in range(TOP):
-                name = f"by_token{piece - 2}" if r == 0 and piece in PACED else f"product{piece}_{r}"
-                product = sbuf.tile([P, width], F32, name=name)
-                cuts = (t0, t0 + CUT, t1) if CUT and piece == CUT_PIECE and r == TOP - 1 else (t0, t1)
-                for c0, c1 in zip(cuts, cuts[1:]):
-                    picks = pos_sb[r][:, c0 // LIST_ROWS : c1 // LIST_ROWS]
-                    nc.vector.tensor_tensor(product[:, c0 - t0 : c1 - t0], y[half][:].indirect(picks), gate_sb[:, r, c0:c1], MULT)
-                products.append(product)
-            out_piece = out[half * P : (half + 1) * P, t0:t1]
-            if (half, t0, t1) == COMBINE_PIECES[-1]:
-                parts = [slice(c0, c0 + LAST_PART) for c0 in range(0, width, LAST_PART)]
-                for part in parts:
-                    nc.vector.tensor_tensor(products[0][:, part], products[0][:, part], products[1][:, part], ADD)
-                for part in parts:
-                    nc.vector.tensor_tensor(products[2][:, part], products[0][:, part], products[2][:, part], ADD)
-                    nc.sync.dma_start(out=out_piece[:, part], in_=products[2][:, part])
-                continue
-            sums = [bank(number, P) for number in SUM_BANKS[piece]]
-            for r in range(TOP):
-                for j, summed in enumerate(sums):
-                    nc.tensor.matmul(
-                        summed[:],
-                        lhsT=products[r][:, j * P : (j + 1) * P],
-                        rhs=ident[:],
-                        is_transpose=True,
-                        start=(r == 0),
-                        stop=(r == TOP - 1),
-                    )
-            by_token = sbuf.tile([P, width], F32, name=f"by_token{piece}")
-            for j, summed in enumerate(sums):
-                nc.scalar.copy(by_token[:, j * P : (j + 1) * P], summed[:])
-            for c0, c1, number in BACK_BANKS[piece]:
-                back = bank(number, c1 - c0)
-                for c in range(c0, c1, P):
-                    nc.tensor.transpose(back[:, c - c0 : c - c0 + P], by_token[:, c : c + P], ident[:])
-                result = sbuf.tile([P, c1 - c0], F32, name=f"result{piece}_{c0}")
+        def picked(half, r, t0, t1):
+            return y[half][:].indirect(pos_sb[r][:, t0 // LIST_ROWS : t1 // LIST_ROWS])
+
+        def gated(half, r, t0, t1):
+            product = sbuf.tile([P, t1 - t0], F32, name=f"product{half}_{r}_{t0}")
+            nc.vector.tensor_tensor(product[:], picked(half, r, t0, t1), gate_sb[:, r, t0:t1], MULT)
+            return product[:]
+
+        def fetch(t0, t1):
+            fetched = sbuf.tile([P, 2, t1 - t0], F32, name=f"fetched{t0}")
+            for r in range(2):
+                nc.scalar.activation(fetched[:, r, :], picked(1, r, t0, t1), COPY)
+            return fetched
+
+        def gate_fetched(fetched, t0, t1):
+            products = sbuf.tile([P, 2, t1 - t0], F32, name=f"gated{t0}")
+            nc.vector.tensor_tensor(products[:], fetched[:], gate_sb[:, 0:2, t0:t1], MULT)
+            return [products[:, 0, :], products[:, 1, :]]
+
+        def sum_on_tensor(products, out_piece, queue):
+            width = out_piece.shape[1]
+            starts = range(0, width, SPLIT)
+            sums = [bank(SPLIT)[0] for c0 in starts]
+            for r, product in enumerate(products):
+                for c0, summed in zip(starts, sums):
+                    for c in range(0, SPLIT, P):
+                        nc.tensor.matmul(
+                            summed[:, c : c + P],
+                            lhsT=product[:, c0 + c : c0 + c + P],
+                            rhs=ident[:],
+                            is_transpose=True,
+                            start=(r == 0 and c == 0),
+                            stop=(r == TOP - 1 and c == SPLIT - P),
+                        )
+            by_token = sbuf.tile([P, width], F32, name=f"by_token{width}")
+            for c0, summed in zip(starts, sums):
+                nc.scalar.copy(by_token[:, c0 : c0 + SPLIT], summed[:])
+            for c0 in starts:
+                back = bank(SPLIT)[0]
+                for c in range(0, SPLIT, P):
+                    nc.tensor.transpose(back[:, c : c + P], by_token[:, c0 + c : c0 + c + P], ident[:])
+                result = sbuf.tile([P, SPLIT], F32, name=f"result{width}_{c0}")
                 nc.scalar.copy(result[:], back[:])
-                (nc.scalar if piece >= OWN_STORES else nc.sync).dma_start(out=out_piece[:, c0:c1], in_=result[:])
+                queue.dma_start(out=out_piece[:, c0 : c0 + SPLIT], in_=result[:])
+
+        early, late = fetch(0, SPLIT), fetch(SPLIT, T)
+        sum_on_tensor([gated(0, r, 0, T) for r in range(TOP)], out[0:P, :], nc.sync)
+        sum_on_tensor(gate_fetched(early, 0, SPLIT) + [gated(1, 2, 0, SPLIT)], out[P:N, 0:SPLIT], nc.scalar)
+        third = gated(1, 2, SPLIT, T)
+        first, second = gate_fetched(late, SPLIT, T)
+        parts = [slice(c0, c0 + LAST_PART) for c0 in range(0, T - SPLIT, LAST_PART)]
+        for part in parts:
+            nc.vector.tensor_tensor(third[:, part], third[:, part], first[:, part], ADD)
+        for part in parts:
+            nc.vector.tensor_tensor(third[:, part], third[:, part], second[:, part], ADD)
+            nc.sync.dma_start(out=out[P:N, SPLIT:T][:, part], in_=third[:, part])

@@ -217,11 +217,9 @@ def tile_moe_pkd_mlp_relu_kernel(
             )
 
         y = [sbuf.tile([P, S], F32, name=f"y{half}") for half in range(2)]
-        second_banks = []
         for half in range(2):
             for run, (first, end) in enumerate(PAIRS):
-                acc, number = bank((end - first) * C, second_banks[-2] if half and run else None)
-                second_banks.append(number)
+                acc = bank((end - first) * C)[0]
                 for e in range(first, end):
                     col = e * N + half * P
                     nc.tensor.matmul_mx(
@@ -255,35 +253,44 @@ def tile_moe_pkd_mlp_relu_kernel(
             nc.vector.tensor_tensor(products[:], fetched[:], gate_sb[:, 0:2, t0:t1], MULT)
             return [products[:, 0, :], products[:, 1, :]]
 
-        def sum_on_tensor(products, out_piece, queue):
-            width = out_piece.shape[1]
-            starts = range(0, width, SPLIT)
-            sums = [bank(SPLIT)[0] for c0 in starts]
+        def add_up(products, pieces):
+            sums = [bank(t1 - t0)[0] for t0, t1 in pieces]
             for r, product in enumerate(products):
-                for c0, summed in zip(starts, sums):
-                    for c in range(0, SPLIT, P):
+                for (t0, t1), summed in zip(pieces, sums):
+                    for c in range(t0, t1, P):
                         nc.tensor.matmul(
-                            summed[:, c : c + P],
-                            lhsT=product[:, c0 + c : c0 + c + P],
+                            summed[:, c - t0 : c - t0 + P],
+                            lhsT=product[:, c : c + P],
                             rhs=ident[:],
                             is_transpose=True,
-                            start=(r == 0 and c == 0),
-                            stop=(r == TOP - 1 and c == SPLIT - P),
+                            start=(r == 0 and c == t0),
+                            stop=(r == TOP - 1 and c == t1 - P),
                         )
-            by_token = sbuf.tile([P, width], F32, name=f"by_token{width}")
-            for c0, summed in zip(starts, sums):
-                nc.scalar.copy(by_token[:, c0 : c0 + SPLIT], summed[:])
-            for c0 in starts:
-                back = bank(SPLIT)[0]
-                for c in range(0, SPLIT, P):
-                    nc.tensor.transpose(back[:, c : c + P], by_token[:, c0 + c : c0 + c + P], ident[:])
-                result = sbuf.tile([P, SPLIT], F32, name=f"result{width}_{c0}")
-                nc.scalar.copy(result[:], back[:])
-                queue.dma_start(out=out_piece[:, c0 : c0 + SPLIT], in_=result[:])
+            return sums
+
+        def turn_back(summed, half, t0, t1):
+            by_token = sbuf.tile([P, t1 - t0], F32, name=f"by_token{half}_{t0}")
+            nc.scalar.copy(by_token[:], summed[:])
+            back = bank(t1 - t0)[0]
+            for c in range(0, t1 - t0, P):
+                nc.tensor.transpose(back[:, c : c + P], by_token[:, c : c + P], ident[:])
+            return back
+
+        def store(back, half, t0, t1, queue):
+            result = sbuf.tile([P, t1 - t0], F32, name=f"result{half}_{t0}")
+            nc.scalar.copy(result[:], back[:])
+            queue.dma_start(out=out[half * P : (half + 1) * P, t0:t1], in_=result[:])
 
         early, late = fetch(0, SPLIT), fetch(SPLIT, T)
-        sum_on_tensor([gated(0, r, 0, T) for r in range(TOP)], out[0:P, :], nc.sync)
-        sum_on_tensor(gate_fetched(early, 0, SPLIT) + [gated(1, 2, 0, SPLIT)], out[P:N, 0:SPLIT], nc.scalar)
+        pieces = ((0, T // 2), (T // 2, T))
+        sums = add_up([gated(0, r, 0, T) for r in range(TOP)], pieces)
+        backs = [turn_back(summed, 0, t0, t1) for summed, (t0, t1) in zip(sums, pieces)]
+        store(backs[0], 0, *pieces[0], nc.sync)
+        third = gated(1, 2, 0, SPLIT)
+        summed = add_up([third] + gate_fetched(early, 0, SPLIT), ((0, SPLIT),))[0]
+        back = turn_back(summed, 1, 0, SPLIT)
+        store(backs[1], 0, *pieces[1], nc.sync)
+        store(back, 1, 0, SPLIT, nc.scalar)
         third = gated(1, 2, SPLIT, T)
         first, second = gate_fetched(late, SPLIT, T)
         parts = [slice(c0, c0 + LAST_PART) for c0 in range(0, T - SPLIT, LAST_PART)]

@@ -216,7 +216,16 @@ def tile_moe_pkd_mlp_relu_kernel(
                 in_=h_by_i[:, first * PACK * C : end * PACK * C],
             )
 
-        y = [sbuf.tile([P, S], F32, name=f"y{half}") for half in range(2)]
+        y = [sbuf.tile([P, S], F32, name=name, align_bytes=64) for name in ("y0", "h_by_i")]
+
+        def picked(half, r, t0, t1):
+            return y[half][:].indirect(pos_sb[r][:, t0 // LIST_ROWS : t1 // LIST_ROWS])
+
+        def fetch(half, t0, t1):
+            values = sbuf.tile([P, t1 - t0], F32, name=f"fetched{half}_{t0}")
+            nc.scalar.activation(values[:], picked(half, 0, t0, t1), COPY)
+            return values[:]
+
         for half in range(2):
             for run, (first, end) in enumerate(PAIRS):
                 acc = bank((end - first) * C)[0]
@@ -233,25 +242,17 @@ def tile_moe_pkd_mlp_relu_kernel(
                     )
                 copy = nc.vector.tensor_copy if half == 0 and run in VECTOR_RUNS else nc.scalar.copy
                 copy(y[half][:, first * C : end * C], acc[:])
+            if half == 0:
+                fetched = fetch(0, 0, T)
 
-        def picked(half, r, t0, t1):
-            return y[half][:].indirect(pos_sb[r][:, t0 // LIST_ROWS : t1 // LIST_ROWS])
-
-        def gated(half, r, t0, t1):
+        def gated(source, half, r, t0, t1):
             product = sbuf.tile([P, t1 - t0], F32, name=f"product{half}_{r}_{t0}")
-            nc.vector.tensor_tensor(product[:], picked(half, r, t0, t1), gate_sb[:, r, t0:t1], MULT)
+            nc.vector.tensor_tensor(product[:], source, gate_sb[:, r, t0:t1], MULT)
             return product[:]
 
-        def fetch(t0, t1):
-            fetched = sbuf.tile([P, 2, t1 - t0], F32, name=f"fetched{t0}")
-            for r in range(2):
-                nc.scalar.activation(fetched[:, r, :], picked(1, r, t0, t1), COPY)
-            return fetched
-
-        def gate_fetched(fetched, t0, t1):
-            products = sbuf.tile([P, 2, t1 - t0], F32, name=f"gated{t0}")
-            nc.vector.tensor_tensor(products[:], fetched[:], gate_sb[:, 0:2, t0:t1], MULT)
-            return [products[:, 0, :], products[:, 1, :]]
+        def products(values, half, t0, t1):
+            gathered = [gated(picked(half, r, t0, t1), half, r, t0, t1) for r in (1, 2)]
+            return gathered + [gated(values, half, 0, t0, t1)]
 
         def add_up(products, pieces):
             sums = [bank(t1 - t0)[0] for t0, t1 in pieces]
@@ -281,21 +282,20 @@ def tile_moe_pkd_mlp_relu_kernel(
             nc.scalar.copy(result[:], back[:])
             queue.dma_start(out=out[half * P : (half + 1) * P, t0:t1], in_=result[:])
 
-        early, late = fetch(0, SPLIT), fetch(SPLIT, T)
         pieces = ((0, T // 2), (T // 2, T))
-        sums = add_up([gated(0, r, 0, T) for r in range(TOP)], pieces)
+        sums = add_up(products(fetched, 0, 0, T), pieces)
+        early = fetch(1, 0, SPLIT)
         backs = [turn_back(summed, 0, t0, t1) for summed, (t0, t1) in zip(sums, pieces)]
+        late = fetch(1, SPLIT, T)
+        summed = add_up(products(early, 1, 0, SPLIT), ((0, SPLIT),))[0]
         store(backs[0], 0, *pieces[0], nc.sync)
-        third = gated(1, 2, 0, SPLIT)
-        summed = add_up([third] + gate_fetched(early, 0, SPLIT), ((0, SPLIT),))[0]
         back = turn_back(summed, 1, 0, SPLIT)
         store(backs[1], 0, *pieces[1], nc.sync)
         store(back, 1, 0, SPLIT, nc.scalar)
-        third = gated(1, 2, SPLIT, T)
-        first, second = gate_fetched(late, SPLIT, T)
+        second, third, first = products(late, 1, SPLIT, T)
         parts = [slice(c0, c0 + LAST_PART) for c0 in range(0, T - SPLIT, LAST_PART)]
         for part in parts:
-            nc.vector.tensor_tensor(third[:, part], third[:, part], first[:, part], ADD)
-        for part in parts:
             nc.vector.tensor_tensor(third[:, part], third[:, part], second[:, part], ADD)
+        for part in parts:
+            nc.vector.tensor_tensor(third[:, part], third[:, part], first[:, part], ADD)
             nc.sync.dma_start(out=out[P:N, SPLIT:T][:, part], in_=third[:, part])

@@ -37,8 +37,8 @@ PERMUTE_RUNS = ((TURNED, EARLY), (EARLY, LATE), (LATE, E - 1), (E - 1, E))
 PAIRS = tuple((e, min(e + 2, E)) for e in range(0, E, 2))
 VECTOR_EXPERT = 6
 VECTOR_RUNS = (2, 4)
-SPLIT = 384
-LAST_PART = 192
+SPLIT = 256
+LAST = 512
 
 
 def tile_moe_pkd_mlp_relu_kernel(
@@ -221,9 +221,9 @@ def tile_moe_pkd_mlp_relu_kernel(
         def picked(half, r, t0, t1):
             return y[half][:].indirect(pos_sb[r][:, t0 // LIST_ROWS : t1 // LIST_ROWS])
 
-        def fetch(half, t0, t1):
-            values = sbuf.tile([P, t1 - t0], F32, name=f"fetched{half}_{t0}")
-            nc.scalar.activation(values[:], picked(half, 0, t0, t1), COPY)
+        def fetch(half, t0, t1, r=0, buffer=None):
+            values = sbuf.tile([P, t1 - t0], F32, name=buffer or f"fetched{half}_{r}_{t0}")
+            nc.scalar.activation(values[:], picked(half, r, t0, t1), COPY)
             return values[:]
 
         for half in range(2):
@@ -244,6 +244,7 @@ def tile_moe_pkd_mlp_relu_kernel(
                 copy(y[half][:, first * C : end * C], acc[:])
             if half == 0:
                 fetched = fetch(0, 0, T)
+
 
         def gated(source, half, r, t0, t1):
             product = sbuf.tile([P, t1 - t0], F32, name=f"product{half}_{r}_{t0}")
@@ -285,17 +286,23 @@ def tile_moe_pkd_mlp_relu_kernel(
         pieces = ((0, T // 2), (T // 2, T))
         sums = add_up(products(fetched, 0, 0, T), pieces)
         early = fetch(1, 0, SPLIT)
-        backs = [turn_back(summed, 0, t0, t1) for summed, (t0, t1) in zip(sums, pieces)]
         late = fetch(1, SPLIT, T)
+        backs = [turn_back(summed, 0, t0, t1) for summed, (t0, t1) in zip(sums, pieces)]
+        last = fetch(1, LAST, T, 1, "product0_0_0")
         summed = add_up(products(early, 1, 0, SPLIT), ((0, SPLIT),))[0]
-        store(backs[0], 0, *pieces[0], nc.sync)
         back = turn_back(summed, 1, 0, SPLIT)
+        store(backs[0], 0, *pieces[0], nc.sync)
         store(backs[1], 0, *pieces[1], nc.sync)
         store(back, 1, 0, SPLIT, nc.scalar)
-        second, third, first = products(late, 1, SPLIT, T)
-        parts = [slice(c0, c0 + LAST_PART) for c0 in range(0, T - SPLIT, LAST_PART)]
-        for part in parts:
-            nc.vector.tensor_tensor(third[:, part], third[:, part], second[:, part], ADD)
-        for part in parts:
-            nc.vector.tensor_tensor(third[:, part], third[:, part], first[:, part], ADD)
-            nc.sync.dma_start(out=out[P:N, SPLIT:T][:, part], in_=third[:, part])
+
+        third = gated(picked(1, 2, SPLIT, T), 1, 2, SPLIT, T)
+        second = gated(picked(1, 1, SPLIT, LAST), 1, 1, SPLIT, LAST)
+        first = gated(late, 1, 0, SPLIT, T)
+        seconds = (second, gated(last, 1, 1, LAST, T))
+        parts = ((SPLIT, LAST), (LAST, T))
+        totals = [third[:, t0 - SPLIT : t1 - SPLIT] for t0, t1 in parts]
+        for total, (t0, t1) in zip(totals, parts):
+            nc.vector.tensor_tensor(total, total, first[:, t0 - SPLIT : t1 - SPLIT], ADD)
+        for total, second, (t0, t1) in zip(totals, seconds, parts):
+            nc.vector.tensor_tensor(total, total, second, ADD)
+            nc.sync.dma_start(out=out[P:N, t0:t1], in_=total)

@@ -37,8 +37,9 @@ PERMUTE_RUNS = ((TURNED, EARLY), (EARLY, LATE), (LATE, E - 1), (E - 1, E))
 PAIRS = tuple((e, min(e + 2, E)) for e in range(0, E, 2))
 VECTOR_EXPERT = 6
 VECTOR_RUNS = (2, 4)
-SPLIT = 256
-LAST = 512
+CUT0 = 512
+CUT1 = 256
+GATE_ROWS = 64
 
 
 def tile_moe_pkd_mlp_relu_kernel(
@@ -64,7 +65,10 @@ def tile_moe_pkd_mlp_relu_kernel(
         w1_plane_early = sbuf.tile([P, EARLY * H], U8, name="w1_plane_early", align_bytes=64)
         w1_plane_late = sbuf.tile([P, (E - EARLY) * H], U8, name="w1_plane_late", align_bytes=64)
         w2_plane = sbuf.tile([P, E * N], U8, name="w2_plane", align_bytes=64)
-        gate_sb = sbuf.tile([P, TOP, T], F32, name="gate_sb")
+        gate_first = sbuf.tile([P, T - CUT1], F32, name="gate_first")
+        gate_later = sbuf.tile([P, TOP - 1, T], F32, name="gate_later")
+        gate_rows = sbuf.tile([P, P], F32, name="gate_rows")
+        gate_by_token = sbuf.tile([P, TOP - 1, T // P], F32, name="gate_by_token")
         ident = sbuf.tile([P, P], F32, name="ident")
 
         for plane in (w1_plane_early, w1_plane_late, w2_plane):
@@ -103,7 +107,11 @@ def tile_moe_pkd_mlp_relu_kernel(
         w2_tile = load_words(w2_words, slice(0, E), "w2_tile")
         for r, pos in enumerate((pos1, pos2, pos3)):
             nc.sync.dma_start(pos_sb[r][:], pos)
-        nc.sync.dma_start(out=gate_sb[:], in_=gate[:, 0:P, :].rearrange("r p t -> p r t"))
+        nc.sync.dma_start(
+            out=gate_rows[:], in_=gate[0 : TOP - 1].rearrange("r n (c t) -> r (n c) t", t=P)[:, 0:GATE_ROWS, :]
+        )
+        nc.sync.dma_start(out=gate_later[:], in_=gate[1:TOP, 0:P, :].rearrange("r p t -> p r t"))
+        nc.sync.dma_start(out=gate_first[:], in_=gate[0, 0:P, CUT1:T])
 
         def w1_as_loaded(first, end):
             loads = ((w1_late, LATE, LATE), (w1_early, EARLY, EARLY), (w1_first, 0, 0))
@@ -217,15 +225,6 @@ def tile_moe_pkd_mlp_relu_kernel(
             )
 
         y = [sbuf.tile([P, S], F32, name=name, align_bytes=64) for name in ("y0", "h_by_i")]
-
-        def picked(half, r, t0, t1):
-            return y[half][:].indirect(pos_sb[r][:, t0 // LIST_ROWS : t1 // LIST_ROWS])
-
-        def fetch(half, t0, t1, r=0, buffer=None):
-            values = sbuf.tile([P, t1 - t0], F32, name=buffer or f"fetched{half}_{r}_{t0}")
-            nc.scalar.activation(values[:], picked(half, r, t0, t1), COPY)
-            return values[:]
-
         for half in range(2):
             for run, (first, end) in enumerate(PAIRS):
                 acc = bank((end - first) * C)[0]
@@ -242,67 +241,98 @@ def tile_moe_pkd_mlp_relu_kernel(
                     )
                 copy = nc.vector.tensor_copy if half == 0 and run in VECTOR_RUNS else nc.scalar.copy
                 copy(y[half][:, first * C : end * C], acc[:])
-            if half == 0:
-                fetched = fetch(0, 0, T)
 
+        gate_turned = bank(P)[0]
+        nc.tensor.transpose(gate_turned[:], gate_rows[:], ident[:])
+        nc.scalar.copy(gate_by_token[:], gate_turned[:].rearrange("p (r c) -> p r c", r=TOP - 1)[:, :, 0 : T // P])
 
-        def gated(source, half, r, t0, t1):
+        def picked(half, r, t0, t1):
+            return y[half][:].indirect(pos_sb[r][:, t0 // LIST_ROWS : t1 // LIST_ROWS])
+
+        def fetch(half, r, t0, t1):
+            values = sbuf.tile([P, t1 - t0], F32, name=f"fetched{half}_{r}_{t0}")
+            nc.scalar.activation(values[:], picked(half, r, t0, t1), COPY)
+            return values[:]
+
+        def gated(half, r, t0, t1):
             product = sbuf.tile([P, t1 - t0], F32, name=f"product{half}_{r}_{t0}")
-            nc.vector.tensor_tensor(product[:], source, gate_sb[:, r, t0:t1], MULT)
+            weights = gate_later[:, r - 1, t0:t1] if r else gate_first[:, t0 - CUT1 : t1 - CUT1]
+            nc.vector.tensor_tensor(product[:], picked(half, r, t0, t1), weights, MULT)
             return product[:]
 
-        def products(values, half, t0, t1):
-            gathered = [gated(picked(half, r, t0, t1), half, r, t0, t1) for r in (1, 2)]
-            return gathered + [gated(values, half, 0, t0, t1)]
+        def turn_side_by_side(parts):
+            turned = bank(sum(values.shape[1] for values in parts))[0]
+            at = 0
+            for values in parts:
+                for c in range(0, values.shape[1], P):
+                    nc.tensor.transpose(turned[:, at : at + P], values[:, c : c + P], ident[:])
+                    at = at + P
+            return turned[:]
 
-        def add_up(products, pieces):
-            sums = [bank(t1 - t0)[0] for t0, t1 in pieces]
-            for r, product in enumerate(products):
-                for (t0, t1), summed in zip(pieces, sums):
-                    for c in range(t0, t1, P):
-                        nc.tensor.matmul(
-                            summed[:, c - t0 : c - t0 + P],
-                            lhsT=product[:, c : c + P],
-                            rhs=ident[:],
-                            is_transpose=True,
-                            start=(r == 0 and c == t0),
-                            stop=(r == TOP - 1 and c == t1 - P),
-                        )
-            return sums
-
-        def turn_back(summed, half, t0, t1):
-            by_token = sbuf.tile([P, t1 - t0], F32, name=f"by_token{half}_{t0}")
-            nc.scalar.copy(by_token[:], summed[:])
-            back = bank(t1 - t0)[0]
+        def scale(turned, half, r, t0, t1):
+            scaled = sbuf.tile([P, t1 - t0], F32, name=f"scaled{half}_{r}_{t0}")
             for c in range(0, t1 - t0, P):
-                nc.tensor.transpose(back[:, c : c + P], by_token[:, c : c + P], ident[:])
-            return back
+                block = (t0 + c) // P
+                nc.scalar.activation(
+                    scaled[:, c : c + P], turned[:, c : c + P], COPY, scale=gate_by_token[:, r, block : block + 1]
+                )
+            return scaled[:]
 
-        def store(back, half, t0, t1, queue):
+        def add_turned(summed, term, first, last):
+            width = term.shape[1]
+            for c in range(0, width, P):
+                nc.tensor.matmul(
+                    summed[:, c : c + P],
+                    lhsT=term[:, c : c + P],
+                    rhs=ident[:],
+                    is_transpose=True,
+                    start=(first and c == 0),
+                    stop=(last and c == width - P),
+                )
+
+        def finish(summed, product, half, t0, t1):
             result = sbuf.tile([P, t1 - t0], F32, name=f"result{half}_{t0}")
-            nc.scalar.copy(result[:], back[:])
-            queue.dma_start(out=out[half * P : (half + 1) * P, t0:t1], in_=result[:])
+            nc.vector.tensor_tensor(result[:], summed[:], product, ADD)
+            nc.sync.dma_start(out=out[half * P : (half + 1) * P, t0:t1], in_=result[:])
 
-        pieces = ((0, T // 2), (T // 2, T))
-        sums = add_up(products(fetched, 0, 0, T), pieces)
-        early = fetch(1, 0, SPLIT)
-        late = fetch(1, SPLIT, T)
-        backs = [turn_back(summed, 0, t0, t1) for summed, (t0, t1) in zip(sums, pieces)]
-        last = fetch(1, LAST, T, 1, "product0_0_0")
-        summed = add_up(products(early, 1, 0, SPLIT), ((0, SPLIT),))[0]
-        back = turn_back(summed, 1, 0, SPLIT)
-        store(backs[0], 0, *pieces[0], nc.sync)
-        store(backs[1], 0, *pieces[1], nc.sync)
-        store(back, 1, 0, SPLIT, nc.scalar)
+        second0 = gated(0, 1, 0, CUT0)
+        third0 = gated(0, 2, 0, T)
+        third1 = gated(1, 2, 0, T)
+        second1 = gated(1, 1, CUT1, T)
+        first1 = gated(1, 0, CUT1, T)
 
-        third = gated(picked(1, 2, SPLIT, T), 1, 2, SPLIT, T)
-        second = gated(picked(1, 1, SPLIT, LAST), 1, 1, SPLIT, LAST)
-        first = gated(late, 1, 0, SPLIT, T)
-        seconds = (second, gated(last, 1, 1, LAST, T))
-        parts = ((SPLIT, LAST), (LAST, T))
-        totals = [third[:, t0 - SPLIT : t1 - SPLIT] for t0, t1 in parts]
+        pair_sum = bank(CUT0)[0]
+        add_turned(pair_sum, second0, True, False)
+        add_turned(pair_sum, third0[:, 0:CUT0], False, True)
+        fetched_first0 = fetch(0, 0, 0, T)
+        fetched_second0 = fetch(0, 1, CUT0, T)
+        fetched1 = [fetch(1, r, 0, CUT1) for r in range(2)]
+        pair_by_token = sbuf.tile([P, CUT0], F32, name="pair_by_token")
+        nc.scalar.copy(pair_by_token[:], pair_sum[:])
+        short0 = turn_side_by_side([fetched_first0[:, CUT0:T], fetched_second0])
+        wide0 = turn_side_by_side([fetched_first0[:, 0:CUT0]])
+        short1 = turn_side_by_side(fetched1)
+        wide_sum = bank(CUT0)[0]
+        add_turned(wide_sum, pair_by_token[:], True, False)
+
+        short_sum0 = bank(T - CUT0)[0]
+        for r in range(2):
+            add_turned(short_sum0, scale(short0[:, r * (T - CUT0) : (r + 1) * (T - CUT0)], 0, r, CUT0, T), r == 0, r == 1)
+        add_turned(wide_sum, scale(wide0, 0, 0, 0, CUT0), False, True)
+        short_sum1 = bank(CUT1)[0]
+        for r in range(2):
+            add_turned(short_sum1, scale(short1[:, r * CUT1 : (r + 1) * CUT1], 1, r, 0, CUT1), r == 0, r == 1)
+
+        middle = (CUT1 + T) // 2
+        parts = ((CUT1, middle), (middle, T))
+        totals = [third1[:, t0:t1] for t0, t1 in parts]
         for total, (t0, t1) in zip(totals, parts):
-            nc.vector.tensor_tensor(total, total, first[:, t0 - SPLIT : t1 - SPLIT], ADD)
-        for total, second, (t0, t1) in zip(totals, seconds, parts):
-            nc.vector.tensor_tensor(total, total, second, ADD)
+            nc.vector.tensor_tensor(total, total, second1[:, t0 - CUT1 : t1 - CUT1], ADD)
+        finish(short_sum0, third0[:, CUT0:T], 0, CUT0, T)
+        for total, (t0, t1) in zip(totals, parts):
+            nc.vector.tensor_tensor(total, total, first1[:, t0 - CUT1 : t1 - CUT1], ADD)
             nc.sync.dma_start(out=out[P:N, t0:t1], in_=total)
+        wide_result = sbuf.tile([P, CUT0], F32, name="wide_result")
+        nc.scalar.copy(wide_result[:], wide_sum[:])
+        nc.scalar.dma_start(out=out[0:P, 0:CUT0], in_=wide_result[:])
+        finish(short_sum1, third1[:, 0:CUT1], 1, 0, CUT1)

@@ -37,9 +37,7 @@ PERMUTE_RUNS = ((TURNED, EARLY), (EARLY, LATE), (LATE, E - 1), (E - 1, E))
 PAIRS = tuple((e, min(e + 2, E)) for e in range(0, E, 2))
 VECTOR_EXPERT = 6
 VECTOR_RUNS = (2, 4)
-CUT0 = 512
-CUT1 = 256
-GATE_ROWS = 64
+CUT = 512
 
 
 def tile_moe_pkd_mlp_relu_kernel(
@@ -65,10 +63,9 @@ def tile_moe_pkd_mlp_relu_kernel(
         w1_plane_early = sbuf.tile([P, EARLY * H], U8, name="w1_plane_early", align_bytes=64)
         w1_plane_late = sbuf.tile([P, (E - EARLY) * H], U8, name="w1_plane_late", align_bytes=64)
         w2_plane = sbuf.tile([P, E * N], U8, name="w2_plane", align_bytes=64)
-        gate_first = sbuf.tile([P, T - CUT1], F32, name="gate_first")
-        gate_later = sbuf.tile([P, TOP - 1, T], F32, name="gate_later")
+        gate_sb = sbuf.tile([P, TOP, CUT], F32, name="gate_sb")
         gate_rows = sbuf.tile([P, P], F32, name="gate_rows")
-        gate_by_token = sbuf.tile([P, TOP - 1, T // P], F32, name="gate_by_token")
+        gate_by_token = sbuf.tile([P, TOP, (T - CUT) // P], F32, name="gate_by_token")
         ident = sbuf.tile([P, P], F32, name="ident")
 
         for plane in (w1_plane_early, w1_plane_late, w2_plane):
@@ -76,6 +73,7 @@ def tile_moe_pkd_mlp_relu_kernel(
         nc.vector.memset(x_word_tile[:, T:WINDOW], 0)
         nc.vector.memset(x_plane[:].bitcast(I32)[:, T // 4 : WINDOW // 4], 0)
         make_identity(nc, ident[:])
+        nc.gpsimd.memset(gate_rows[:], 0.0)
 
         def load_plane(plane, scales, first, end):
             for r in range(4):
@@ -107,11 +105,11 @@ def tile_moe_pkd_mlp_relu_kernel(
         w2_tile = load_words(w2_words, slice(0, E), "w2_tile")
         for r, pos in enumerate((pos1, pos2, pos3)):
             nc.sync.dma_start(pos_sb[r][:], pos)
-        nc.sync.dma_start(
-            out=gate_rows[:], in_=gate[0 : TOP - 1].rearrange("r n (c t) -> r (n c) t", t=P)[:, 0:GATE_ROWS, :]
-        )
-        nc.sync.dma_start(out=gate_later[:], in_=gate[1:TOP, 0:P, :].rearrange("r p t -> p r t"))
-        nc.sync.dma_start(out=gate_first[:], in_=gate[0, 0:P, CUT1:T])
+        nc.sync.dma_start(out=gate_sb[:], in_=gate[:, 0:P, 0:CUT].rearrange("r p t -> p r t"))
+        blocks = (T - CUT) // P
+        for r0, r1 in ((0, 2), (2, TOP)):
+            rows = gate[r0:r1, 0, CUT:T].rearrange("r (c t) -> r c t", t=P)
+            nc.sync.dma_start(out=gate_rows[r0 * blocks : r1 * blocks, :], in_=rows)
 
         def w1_as_loaded(first, end):
             loads = ((w1_late, LATE, LATE), (w1_early, EARLY, EARLY), (w1_first, 0, 0))
@@ -244,7 +242,7 @@ def tile_moe_pkd_mlp_relu_kernel(
 
         gate_turned = bank(P)[0]
         nc.tensor.transpose(gate_turned[:], gate_rows[:], ident[:])
-        nc.scalar.copy(gate_by_token[:], gate_turned[:].rearrange("p (r c) -> p r c", r=TOP - 1)[:, :, 0 : T // P])
+        nc.scalar.copy(gate_by_token[:], gate_turned[:, 0 : TOP * blocks].rearrange("p (r c) -> p r c", r=TOP))
 
         def picked(half, r, t0, t1):
             return y[half][:].indirect(pos_sb[r][:, t0 // LIST_ROWS : t1 // LIST_ROWS])
@@ -256,8 +254,7 @@ def tile_moe_pkd_mlp_relu_kernel(
 
         def gated(half, r, t0, t1):
             product = sbuf.tile([P, t1 - t0], F32, name=f"product{half}_{r}_{t0}")
-            weights = gate_later[:, r - 1, t0:t1] if r else gate_first[:, t0 - CUT1 : t1 - CUT1]
-            nc.vector.tensor_tensor(product[:], picked(half, r, t0, t1), weights, MULT)
+            nc.vector.tensor_tensor(product[:], picked(half, r, t0, t1), gate_sb[:, r, t0:t1], MULT)
             return product[:]
 
         def turn_side_by_side(parts):
@@ -272,7 +269,7 @@ def tile_moe_pkd_mlp_relu_kernel(
         def scale(turned, half, r, t0, t1):
             scaled = sbuf.tile([P, t1 - t0], F32, name=f"scaled{half}_{r}_{t0}")
             for c in range(0, t1 - t0, P):
-                block = (t0 + c) // P
+                block = (t0 + c - CUT) // P
                 nc.scalar.activation(
                     scaled[:, c : c + P], turned[:, c : c + P], COPY, scale=gate_by_token[:, r, block : block + 1]
                 )
@@ -295,44 +292,34 @@ def tile_moe_pkd_mlp_relu_kernel(
             nc.vector.tensor_tensor(result[:], summed[:], product, ADD)
             nc.sync.dma_start(out=out[half * P : (half + 1) * P, t0:t1], in_=result[:])
 
-        second0 = gated(0, 1, 0, CUT0)
-        third0 = gated(0, 2, 0, T)
-        third1 = gated(1, 2, 0, T)
-        second1 = gated(1, 1, CUT1, T)
-        first1 = gated(1, 0, CUT1, T)
+        def add(total, term):
+            nc.vector.tensor_tensor(total, total, term, ADD)
 
-        pair_sum = bank(CUT0)[0]
-        add_turned(pair_sum, second0, True, False)
-        add_turned(pair_sum, third0[:, 0:CUT0], False, True)
-        fetched_first0 = fetch(0, 0, 0, T)
-        fetched_second0 = fetch(0, 1, CUT0, T)
-        fetched1 = [fetch(1, r, 0, CUT1) for r in range(2)]
-        pair_by_token = sbuf.tile([P, CUT0], F32, name="pair_by_token")
-        nc.scalar.copy(pair_by_token[:], pair_sum[:])
-        short0 = turn_side_by_side([fetched_first0[:, CUT0:T], fetched_second0])
-        wide0 = turn_side_by_side([fetched_first0[:, 0:CUT0]])
-        short1 = turn_side_by_side(fetched1)
-        wide_sum = bank(CUT0)[0]
-        add_turned(wide_sum, pair_by_token[:], True, False)
+        short = T - CUT
+        turned = []
+        for half in range(2):
+            values = [fetch(half, r, CUT, T) for r in range(TOP)]
+            turned.append([turn_side_by_side(values[0:2]), turn_side_by_side(values[2:3])])
+        sums = []
+        for half in range(2):
+            sums.append(bank(short)[0])
+            for r in range(TOP):
+                part = turned[half][r // 2][:, (r % 2) * short : (r % 2 + 1) * short]
+                add_turned(sums[half], scale(part, half, r, CUT, T), r == 0, r == TOP - 1)
+        for half in range(2):
+            result = sbuf.tile([P, short], F32, name=f"result{half}")
+            nc.scalar.copy(result[:], sums[half][:])
+            nc.scalar.dma_start(out=out[half * P : (half + 1) * P, CUT:T], in_=result[:])
 
-        short_sum0 = bank(T - CUT0)[0]
-        for r in range(2):
-            add_turned(short_sum0, scale(short0[:, r * (T - CUT0) : (r + 1) * (T - CUT0)], 0, r, CUT0, T), r == 0, r == 1)
-        add_turned(wide_sum, scale(wide0, 0, 0, 0, CUT0), False, True)
-        short_sum1 = bank(CUT1)[0]
-        for r in range(2):
-            add_turned(short_sum1, scale(short1[:, r * CUT1 : (r + 1) * CUT1], 1, r, 0, CUT1), r == 0, r == 1)
-
-        middle = (CUT1 + T) // 2
-        parts = ((CUT1, middle), (middle, T))
-        totals = [third1[:, t0:t1] for t0, t1 in parts]
-        for total, (t0, t1) in zip(totals, parts):
-            nc.vector.tensor_tensor(total, total, second1[:, t0 - CUT1 : t1 - CUT1], ADD)
-        finish(short_sum0, third0[:, CUT0:T], 0, CUT0, T)
-        for total, (t0, t1) in zip(totals, parts):
-            nc.vector.tensor_tensor(total, total, first1[:, t0 - CUT1 : t1 - CUT1], ADD)
-            nc.sync.dma_start(out=out[P:N, t0:t1], in_=total)
-        wide_result = sbuf.tile([P, CUT0], F32, name="wide_result")
-        nc.scalar.copy(wide_result[:], wide_sum[:])
-        nc.scalar.dma_start(out=out[0:P, 0:CUT0], in_=wide_result[:])
-        finish(short_sum1, third1[:, 0:CUT1], 1, 0, CUT1)
+        wide0 = [gated(0, r, 0, CUT) for r in range(TOP)]
+        add(wide0[0], wide0[1])
+        wide1 = [gated(1, 0, 0, CUT)]
+        add(wide0[0], wide0[2])
+        nc.sync.dma_start(out=out[0:P, 0:CUT], in_=wide0[0])
+        wide1.extend(gated(1, r, 0, CUT) for r in (1, 2))
+        parts = ((0, CUT // 2), (CUT // 2, CUT))
+        for t0, t1 in parts:
+            add(wide1[0][:, t0:t1], wide1[1][:, t0:t1])
+        for t0, t1 in parts:
+            add(wide1[0][:, t0:t1], wide1[2][:, t0:t1])
+            nc.sync.dma_start(out=out[P:N, t0:t1], in_=wide1[0][:, t0:t1])

from contextlib import ExitStack

import concourse.mybir as mybir
from concourse.masks import make_identity

K, T, E, C, H, N = 512, 768, 9, 256, 512, 256
TOP = 3
S = E * C
P = 128
PACK = 4
LIST_ROWS = 16
FLOPS = 2 * S * (K * H + H * N)

F32 = mybir.dt.float32
BF16 = mybir.dt.bfloat16
I32 = mybir.dt.int32
U32 = mybir.dt.uint32
U16 = mybir.dt.uint16
U8 = mybir.dt.uint8
FP8X4 = mybir.dt.float8_e4m3fn_x4
FP4X4 = mybir.dt.float4_e2m1fn_x4
RELU = mybir.ActivationFunctionType.Relu
MULT = mybir.AluOpType.mult
ADD = mybir.AluOpType.add

COPY = mybir.ActivationFunctionType.Copy

BLOCKS = S // P
BANKS = 8
WINDOW = 1024
WIDEST = 3 * WINDOW // (4 * P)
FIRST_BYTES = 4
GATHER_BUFFERS = 4
TURNED = 2
EARLY, LATE = 3, 6
PERMUTE_RUNS = ((TURNED, EARLY), (EARLY, LATE), (LATE, E - 1), (E - 1, E))
PAIRS = tuple((e, min(e + 2, E)) for e in range(0, E, 2))
VECTOR_EXPERT = 6
VECTOR_RUNS = (2, 4)
CUT = 512


def tile_moe_pkd_mlp_relu_kernel(
    tc, x_words, x_scales, w1_words, w1_scales, w2_words, w2_scales, gate, offs, pos1, pos2, pos3, out
):
    nc = tc.nc
    with ExitStack() as ctx:
        sbuf = ctx.enter_context(tc.tile_pool(name="sbuf", bufs=1))
        psum = ctx.enter_context(tc.psum_pool(name="psum", bufs=1))

        by_age = list(range(BANKS))

        def bank(width, number=None):
            number = by_age[0] if number is None else number
            by_age.remove(number)
            by_age.append(number)
            return psum.tile([P, width], F32, name=f"bank{number}"), number

        offs_sb = sbuf.tile([P, S // LIST_ROWS], U16, name="offs_sb")
        pos_sb = [sbuf.tile([P, T // LIST_ROWS], U16, name=f"pos_sb{r}") for r in range(TOP)]
        x_word_tile = sbuf.tile([P, WINDOW], I32, name="x_word_tile", align_bytes=64)
        x_plane = sbuf.tile([P, WINDOW], U8, name="x_plane", align_bytes=64)
        w1_plane_early = sbuf.tile([P, EARLY * H], U8, name="w1_plane_early", align_bytes=64)
        w1_plane_late = sbuf.tile([P, (E - EARLY) * H], U8, name="w1_plane_late", align_bytes=64)
        w2_plane = sbuf.tile([P, E * N], U8, name="w2_plane", align_bytes=64)
        gate_sb = sbuf.tile([P, TOP, CUT], F32, name="gate_sb")
        gate_rows = sbuf.tile([P, P], F32, name="gate_rows")
        gate_by_token = sbuf.tile([P, TOP, (T - CUT) // P], F32, name="gate_by_token")
        ident = sbuf.tile([P, P], F32, name="ident")

        for plane in (w1_plane_early, w1_plane_late, w2_plane):
            nc.gpsimd.memset(plane[:].bitcast(I32), 0)
        nc.vector.memset(x_word_tile[:, T:WINDOW], 0)
        nc.vector.memset(x_plane[:].bitcast(I32)[:, T // 4 : WINDOW // 4], 0)
        make_identity(nc, ident[:])
        nc.gpsimd.memset(gate_rows[:], 0.0)

        def load_plane(plane, scales, first, end):
            for r in range(4):
                nc.sync.dma_start(
                    out=plane[r:P:32, :].bitcast(I32).rearrange("q (e w) -> q e w", e=end - first),
                    in_=scales[first:end, 0, r:16:4, :].rearrange("e q w -> q e w").bitcast(I32),
                )

        def load_words(words, experts, name):
            source = words[experts, 0].rearrange("e p w -> p e w").bitcast(I32)
            tile = sbuf.tile([P, source.shape[1] * words.shape[-1]], U8, name=name, align_bytes=64)
            nc.sync.dma_start(out=tile[:].bitcast(I32).rearrange("p (e w) -> p e w", e=source.shape[1]), in_=source)
            return tile

        nc.sync.dma_start(offs_sb[:], offs)
        for q in range(4):
            rows = x_scales[0, 4 * q : 4 * q + 4, :].bitcast(I32)
            (nc.sync if q < 2 else nc.scalar).dma_start(
                out=x_plane[32 * q : 32 * q + 32, 0:T].bitcast(I32),
                in_=rows.unsqueeze(0).broadcast_to([8, 4, T // 4]),
            )
        nc.sync.dma_start(out=x_word_tile[:, 0:T], in_=x_words[0].rearrange("p t r -> p (t r)").bitcast(I32))
        w1_first = load_words(w1_words, slice(0, EARLY), "w1_first")
        load_plane(w1_plane_early, w1_scales, 0, EARLY)
        w1_early = load_words(w1_words, slice(EARLY, LATE), "w1_early")
        load_plane(w1_plane_late, w1_scales, EARLY, E)
        w1_late = load_words(w1_words, slice(LATE, E), "w1_late")
        load_plane(w2_plane, w2_scales, 0, E)
        w2_tile = load_words(w2_words, slice(0, E), "w2_tile")
        for r, pos in enumerate((pos1, pos2, pos3)):
            nc.sync.dma_start(pos_sb[r][:], pos)
        nc.sync.dma_start(out=gate_sb[:], in_=gate[:, 0:P, 0:CUT].rearrange("r p t -> p r t"))
        blocks = (T - CUT) // P
        for r0, r1 in ((0, 2), (2, TOP)):
            rows = gate[r0:r1, 0, CUT:T].rearrange("r (c t) -> r c t", t=P)
            nc.sync.dma_start(out=gate_rows[r0 * blocks : r1 * blocks, :], in_=rows)

        def w1_as_loaded(first, end):
            loads = ((w1_late, LATE, LATE), (w1_early, EARLY, EARLY), (w1_first, 0, 0))
            words, least, base = [load for load in loads if load[1] <= first][0]
            plane, plane_base = (w1_plane_late, EARLY) if first >= EARLY else (w1_plane_early, 0)
            return (
                words[:, (first - base) * 2 * H : (end - base) * 2 * H],
                plane[:, (first - plane_base) * H : (end - plane_base) * H],
            )

        last_reader = [-1] * GATHER_BUFFERS
        slot_words, slot_bytes = [], []

        def gather(window, dtype, blocks, count):
            start = len(blocks)
            buffer = last_reader.index(min(last_reader))
            last_reader[buffer] = start + count - 1
            tile = sbuf.tile([P, count * P], dtype, name=f"gathered{buffer}", align_bytes=64)
            picks = offs_sb[:, start * P // LIST_ROWS : (start + count) * P // LIST_ROWS]
            nc.vector.tensor_copy(tile[:], window.indirect(picks))
            blocks.extend(tile[:, c * P : (c + 1) * P] for c in range(count))

        def slot_tokens(block):
            if block == len(slot_bytes):
                reach = FIRST_BYTES if block == 0 else min(len(slot_words) + 2, BLOCKS)
                gather(x_plane[:], U8, slot_bytes, reach - block)
            if block == len(slot_words):
                count = WIDEST if block >= WIDEST else 1 + (block + 1) // 2
                gather(x_word_tile[:].bitcast(U32), U32, slot_words, count)
            return slot_words[block].bitcast(FP8X4), slot_bytes[block]

        w1_permuted = {}
        for first, end in PERMUTE_RUNS:
            raw_words, raw_scales = w1_as_loaded(first, end)
            words = sbuf.tile([P, (end - first) * 2 * H], U8, name=f"permuted_words{first}", align_bytes=64)
            scales = sbuf.tile([P, (end - first) * H], U8, name=f"permuted_scales{first}", align_bytes=64)
            for dst, src in ((scales[:], raw_scales), (words[:].bitcast(U16), raw_words.bitcast(U16))):
                nc.gpsimd.tensor_copy(
                    dst.rearrange("p (e t m) -> p e t m", t=PACK, m=P),
                    src.rearrange("p (e m t) -> p e t m", t=PACK, m=P),
                )
            for e in range(first, end):
                j = e - first
                w1_permuted[e] = (words[:, j * 2 * H : (j + 1) * 2 * H], scales[:, j * H : (j + 1) * H])

        h_by_slot = {}
        h_by_i = sbuf.tile([P, PACK * S], BF16, name="h_by_i", align_bytes=64)

        first_banks = {}

        def first_layer(e):
            if e < TURNED:
                h_by_slot[e] = sbuf.tile([P, 2, H], BF16, name=f"h_by_slot{e}", align_bytes=64)
            for b in range(2):
                block = 2 * e + b
                token_words, token_scales = slot_tokens(block)
                acc, first_banks[block] = bank(H, first_banks[block - 2] if e == TURNED else None)
                if e < TURNED:
                    words, scales = w1_as_loaded(e, e + 1)
                    nc.tensor.matmul_mx(
                        out=acc[:],
                        lhsT=token_words,
                        lhsT_scale=token_scales,
                        rhs=words.bitcast(FP4X4),
                        rhs_scale=scales,
                        start=True,
                        stop=True,
                    )
                    dst = h_by_slot[e][:, b, :].rearrange("s (u p d) -> s u p d", u=2, d=2)
                    src = acc[:].rearrange("s (p u d) -> s u p d", u=2, d=2)
                else:
                    words, scales = w1_permuted[e]
                    for t in range(PACK):
                        nc.tensor.matmul_mx(
                            out=acc[:, t * P : (t + 1) * P],
                            lhsT=words[:, 2 * t * P : 2 * (t + 1) * P].bitcast(FP4X4),
                            lhsT_scale=scales[:, t * P : (t + 1) * P],
                            rhs=token_words,
                            rhs_scale=token_scales,
                            start=True,
                            stop=True,
                        )
                    dst = h_by_i[:, block * H : (block + 1) * H].rearrange("p (s t) -> p s t", t=PACK)
                    src = acc[:].rearrange("p (t s) -> p s t", t=PACK)
                if e == VECTOR_EXPERT:
                    nc.vector.tensor_scalar_max(dst, src, 0.0)
                else:
                    nc.scalar.activation(dst, src, RELU)

        def turn(e):
            pairs = h_by_slot[e][:].rearrange("s b i -> s (b i)").bitcast(F32)
            turned = bank(4 * P)[0]
            for j in range(4):
                nc.tensor.transpose(turned[:, j * P : (j + 1) * P], pairs[:, j * P : (j + 1) * P], ident[:])
            dst = h_by_i[:, e * PACK * C : (e + 1) * PACK * C].bitcast(F32).rearrange("p (b s u) -> p b s u", b=2, u=2)
            nc.scalar.copy(dst, turned[:].rearrange("p (b u s) -> p b s u", b=2, u=2))

        for e in range(E):
            first_layer(e)
            if e == TURNED - 1:
                for done in range(TURNED):
                    turn(done)

        h_words = sbuf.tile([P, S], U32, name="w1_late", align_bytes=64)
        h_plane = sbuf.tile([P, S], U8, name="x_plane", align_bytes=64)
        for first, end in PAIRS:
            nc.vector.quantize_mx(
                out=h_words[:, first * C : end * C].bitcast(FP8X4),
                scales=h_plane[:, first * C : end * C],
                in_=h_by_i[:, first * PACK * C : end * PACK * C],
            )

        y = [sbuf.tile([P, S], F32, name=name, align_bytes=64) for name in ("y0", "h_by_i")]
        for half in range(2):
            for run, (first, end) in enumerate(PAIRS):
                acc = bank((end - first) * C)[0]
                for e in range(first, end):
                    col = e * N + half * P
                    nc.tensor.matmul_mx(
                        out=acc[:, (e - first) * C : (e - first + 1) * C],
                        lhsT=w2_tile[:, 2 * col : 2 * (col + P)].bitcast(FP4X4),
                        lhsT_scale=w2_plane[:, col : col + P],
                        rhs=h_words[:, e * C : (e + 1) * C].bitcast(FP8X4),
                        rhs_scale=h_plane[:, e * C : (e + 1) * C],
                        start=True,
                        stop=True,
                    )
                copy = nc.vector.tensor_copy if half == 0 and run in VECTOR_RUNS else nc.scalar.copy
                copy(y[half][:, first * C : end * C], acc[:])

        gate_turned = bank(P)[0]
        nc.tensor.transpose(gate_turned[:], gate_rows[:], ident[:])
        nc.scalar.copy(gate_by_token[:], gate_turned[:, 0 : TOP * blocks].rearrange("p (r c) -> p r c", r=TOP))

        def picked(half, r, t0, t1):
            return y[half][:].indirect(pos_sb[r][:, t0 // LIST_ROWS : t1 // LIST_ROWS])

        def fetch(half, r, t0, t1):
            values = sbuf.tile([P, t1 - t0], F32, name=f"fetched{half}_{r}_{t0}")
            nc.scalar.activation(values[:], picked(half, r, t0, t1), COPY)
            return values[:]

        def gated(half, r, t0, t1):
            product = sbuf.tile([P, t1 - t0], F32, name=f"product{half}_{r}_{t0}")
            nc.vector.tensor_tensor(product[:], picked(half, r, t0, t1), gate_sb[:, r, t0:t1], MULT)
            return product[:]

        def turn_side_by_side(parts):
            turned = bank(sum(values.shape[1] for values in parts))[0]
            at = 0
            for values in parts:
                for c in range(0, values.shape[1], P):
                    nc.tensor.transpose(turned[:, at : at + P], values[:, c : c + P], ident[:])
                    at = at + P
            return turned[:]

        def scale(turned, half, r, t0, t1):
            scaled = sbuf.tile([P, t1 - t0], F32, name=f"scaled{half}_{r}_{t0}")
            for c in range(0, t1 - t0, P):
                block = (t0 + c - CUT) // P
                nc.scalar.activation(
                    scaled[:, c : c + P], turned[:, c : c + P], COPY, scale=gate_by_token[:, r, block : block + 1]
                )
            return scaled[:]

        def add_turned(summed, term, first, last):
            width = term.shape[1]
            for c in range(0, width, P):
                nc.tensor.matmul(
                    summed[:, c : c + P],
                    lhsT=term[:, c : c + P],
                    rhs=ident[:],
                    is_transpose=True,
                    start=(first and c == 0),
                    stop=(last and c == width - P),
                )

        def finish(summed, product, half, t0, t1):
            result = sbuf.tile([P, t1 - t0], F32, name=f"result{half}_{t0}")
            nc.vector.tensor_tensor(result[:], summed[:], product, ADD)
            nc.sync.dma_start(out=out[half * P : (half + 1) * P, t0:t1], in_=result[:])

        def add(total, term):
            nc.vector.tensor_tensor(total, total, term, ADD)

        short = T - CUT
        turned = []
        for half in range(2):
            values = [fetch(half, r, CUT, T) for r in range(TOP)]
            turned.append([turn_side_by_side(values[0:2]), turn_side_by_side(values[2:3])])
        sums = []
        for half in range(2):
            sums.append(bank(short)[0])
            for r in range(TOP):
                part = turned[half][r // 2][:, (r % 2) * short : (r % 2 + 1) * short]
                add_turned(sums[half], scale(part, half, r, CUT, T), r == 0, r == TOP - 1)
        for half in range(2):
            result = sbuf.tile([P, short], F32, name=f"result{half}")
            nc.scalar.copy(result[:], sums[half][:])
            nc.scalar.dma_start(out=out[half * P : (half + 1) * P, CUT:T], in_=result[:])

        wide0 = [gated(0, r, 0, CUT) for r in range(TOP)]
        add(wide0[0], wide0[1])
        wide1 = [gated(1, 0, 0, CUT)]
        add(wide0[0], wide0[2])
        nc.sync.dma_start(out=out[0:P, 0:CUT], in_=wide0[0])
        wide1.extend(gated(1, r, 0, CUT) for r in (1, 2))
        parts = ((0, CUT // 2), (CUT // 2, CUT))
        for t0, t1 in parts:
            add(wide1[0][:, t0:t1], wide1[1][:, t0:t1])
        for t0, t1 in parts:
            add(wide1[0][:, t0:t1], wide1[2][:, t0:t1])
            nc.sync.dma_start(out=out[P:N, t0:t1], in_=wide1[0][:, t0:t1])
